import numpy as np, ml_dtypes
CORES = [40,41,42,43,44,45,46,47]
N = 8
BF = ml_dtypes.bfloat16
V, R, C, LA, HL, RO, HM = 2048, 128, 5, 256, 64, 2, 2048
Z = V - 1
def climb(fa, v, n):
    for _ in range(n): v = fa[v]
    return v
def mates(rng, fa, dp, a, e):
    key = np.arange(V)
    for _ in range(C): key = np.where(dp[key] > e, fa[key], key)
    o = np.argsort(key[:Z], kind="stable"); ks = key[o]; lo = np.searchsorted(ks, key[a]); hi = np.searchsorted(ks, key[a], side="right")
    return o[lo + (rng.random(a.shape) * (hi - lo)).astype(np.int64)]
def levels(c, top):
    m = V - 1 - R; t = int(np.sum(c)); n = [m * int(i) // t for i in c]; n[0] = min(n[0], top * R)
    for i in range(1, C): n[i] = min(n[i], 14 * n[i - 1])
    n[C - 1] += m - sum(n)
    return n
def forest(rng, n, sp, roots, num, forced):
    kd = np.full((16, V), Z); fa = np.arange(V); dp = np.zeros(V, np.int64); up = roots; pos = 0
    for d in range(C):
        key = rng.exponential(1.0, (len(up), 16)) * np.exp2(rng.integers(-sp, sp + 1, (len(up), 1)))
        for i, (u, j) in enumerate(forced[d] if d < len(forced) else ()): key[u, j] = i - 1000.0
        o = np.argsort(key, axis=None)[:n[d]]; nodes = num[pos:pos + n[d]]; pos += n[d]; u = up[o >> 4]
        kd[o & 15, u] = nodes; fa[nodes] = u; dp[nodes] = d + 1; up = nodes
    return kd, fa, dp
def lanes(rng, fa, dp):
    a = rng.integers(0, Z, LA); b = rng.integers(0, V, LA); p = rng.integers(0, C + 1, LA)
    for e in range(C): b = np.where(p == e, mates(rng, fa, dp, a, e), b)
    return a, b
def base(rng, plan=None):
    kd = np.zeros((N, 8, 16, V), np.int64); fa = np.zeros((N, 8, V), np.int64); dp = fa.copy(); pa = np.zeros((N, 8, LA), np.int64); pb = pa.copy()
    for q in range(N):
        for g in range(8):
            c, top, sp = plan(rng, q, g) if plan else (rng.integers(2, 5, C), 8, 3)
            kd[q, g], fa[q, g], dp[q, g] = forest(rng, levels(c, top), sp, rng.permutation(R), R + rng.permutation(V - 1 - R), ())
            pa[q, g], pb[q, g] = lanes(rng, fa[q, g], dp[q, g])
    x = (rng.random((N, 8, 16, V)) * 256 * np.exp2(rng.integers(-2, 1, (N, 8, 1, V)))).astype(np.int64)
    return dict(x=x, kd=kd, fa=fa, dp=dp, pa=pa, pb=pb, w=rng.integers(0, 256, (N, 8, 16, 1)))
def pack(s):
    x = s["x"].copy(); x[..., Z] = 0; i4 = lambda v, *sh: np.ascontiguousarray(v.reshape(sh)).astype(np.int32)
    return {"xs": np.ascontiguousarray(x.reshape(N, 128, V)).astype(np.float32).astype(BF), "kd": i4(s["kd"], N, 128, V), "fa": i4(s["fa"], N, 8, V), "dp": i4(s["dp"], N, 8, V),
            "pa": i4(s["pa"], N, 8, LA), "pb": i4(s["pb"], N, 8, LA), "wt": i4(s["w"], N, 128, 1)}
def setup_inputs(rng):
    return pack(base(rng))
def setup_inputs_spread(rng):
    s = base(rng, lambda r, q, g: (r.integers(2, 5, C), 8, 6))
    s["x"] = (rng.random((N, 8, 16, V)) * np.exp2(rng.integers(0, 9, (N, 8, 1, V)))).astype(np.int64)
    s["w"] = (rng.random((N, 8, 16, 1)) * np.exp2(rng.integers(0, 9, (N, 8, 16, 1)))).astype(np.int64)
    return pack(s)
def setup_inputs_ends(rng):
    n = [2 * R] + [(36 * V // 100 - 2 * R) // (C - 2)] * (C - 2); n.append(V - 1 - R - sum(n)); s = base(rng)
    forced = ([(0, 0), (0, 15), (1, 0)], [(0, 0), (0, 7), (0, 14), (0, 15), (1, 0), (1, 3), (1, 15)], [(i, j) for i in range(7) for j in (0, 15)])
    k = rng.random((N, 8, 1, V)); x = 255 * rng.integers(0, 2, (N, 8, 16, V)); x = np.where(k < 0.35, 255, np.where(k < 0.6, 0, x)); w = 255 * rng.integers(0, 2, (N, 8, 16, 1))
    for q in range(N):
        for g in range(8):
            num = R + rng.permutation(V - 1 - R)
            for at, v in ((0, V - 3), (1, R), (2, V - 2), (n[0] + 3, V - 4), (n[0], R + 1)):
                j = int(np.flatnonzero(num == v)[0]); num[j] = num[at]; num[at] = v
            kd, fa, dp = forest(rng, n, 3, np.concatenate([np.array([R - 1, 0]), 1 + rng.permutation(R - 2)]), num, forced)
            s["kd"][q, g], s["fa"][q, g], s["dp"][q, g] = kd, fa, dp
            mode = (7 - g + N - 1 - q) % 4; A, B = V - 3, R; y = x[q, g]; fam = []
            for v in (A, B):
                c = kd[:, v]; c = c[c != Z]; t = kd[:, c].reshape(-1); fam.append((c, t[t != Z]))
            y[:, A] = 0; y[:, B] = 0
            for c, t in fam: y[:, c] = 255; y[:, t] = 255
            y[(q + g) % 16, fam[0][0]] = 254
            best = num[n[0] + 1:n[0] + 4] if (q + g) % 2 == 0 else num[n[0] + 3:n[0] + 4]
            y[:, best] = 255
            if mode == 0: w[q, g] = 255
            if mode == 1: y[:, fam[1][0]] = 0; y[:, fam[1][1]] = 0
            if mode == 2: y[:, fam[0][0]] = 0; y[:, fam[0][1]] = 0
            if mode == 3:
                o = rng.permutation(16)[:9]; y[o[:, None], fam[1][0][None]] = 0; y[o[:, None], fam[1][1][None]] = 0
            a, b = lanes(rng, fa, dp); end = rng.random(LA) < 0.72
            a = np.where(end, rng.choice(np.array([0, V - 2]), LA), a); b = np.where(end, rng.choice(np.array([0, Z]), LA), b)
            a = np.where(climb(fa, a, C) == R - 1, 0, a); a[LA - 1] = A; b[LA - 1] = B
            s["pa"][q, g], s["pb"][q, g] = a, b
    s["x"], s["w"] = x, w
    return pack(s)
def setup_inputs_corners(rng):
    def plan(r, q, g):
        return ((r.integers(2, 5, C), 8, 20), ([1] * (C - 1) + [8], 8, 3), ([8] + [1] * (C - 1), 16, 3), (r.integers(2, 5, C), 8, 0))[(q + g) % 4]
    s = base(rng, plan); k = rng.random((N, 8, 1, V)); s["x"] = np.where(k < 0.15, 255, np.where(k < 0.3, 0, s["x"]))
    for q in range(N):
        for g in range(8):
            fa, dp = s["fa"][q, g], s["dp"][q, g]; a = np.where(rng.random(LA) < 0.4, rng.choice(np.array([0, R - 1, R, V - 2]), LA), s["pa"][q, g]); t = rng.integers(0, 5, LA)
            b = np.where(t == 0, rng.choice(np.array([0, R - 1, R, V - 2, Z]), LA), np.where(t == 1, a, np.where(t == 2, fa[a], np.where(t == 3, mates(rng, fa, dp, a, 0), mates(rng, fa, dp, a, C - 2)))))
            s["pa"][q, g], s["pb"][q, g] = a, b
            u = (q + 2 * g) % 5
            if u == 0: s["w"][q, g] = 0
            if u == 1: s["w"][q, g] = 255
    return pack(s)
def setup_inputs_ties(rng):
    s = base(rng)
    for q in range(N):
        for g in range(8):
            m = rng.choice(np.array([0, 0, 0, 8, 9, 16]), V); y = 100 + (rng.permutation(16)[:, None] < m[None]).astype(np.int64); t = rng.random(V)
            if (q + g) % 3: y = np.where(t < 0.12, 0, np.where(t < 0.2, 255, y))
            s["x"][q, g] = y
    return pack(s)
def pairs(rng, s, q, g):
    left = V - 1 - R - 5 * LA; more = left // (C - 2); n = [LA, 2 * LA, 2 * LA + more] + [more] * (C - 3); n[C - 1] += V - 1 - R - sum(n)
    rows = np.argsort(rng.random((LA, 16)), axis=1)[:, :2]; slot = rng.integers(0, 16, 2 * LA); num = R + rng.permutation(V - 1 - R)
    forced = ((), [(i >> 1, int(rows[i >> 1, i & 1])) for i in range(2 * LA)], [(i, int(slot[i])) for i in range(2 * LA)])
    kd, fa, dp = forest(rng, n, 3, rng.permutation(R), num, forced)
    s["kd"][q, g], s["fa"][q, g], s["dp"][q, g] = kd, fa, dp
    at = np.zeros(V, np.int64); at[num[LA:3 * LA]] = np.arange(2 * LA); m = np.flatnonzero(dp == 3); t = at[fa[m]]
    win = rng.integers(0, 2, LA); hi = np.argsort(rng.random((16, LA)), axis=0) < rng.integers(9, 17, LA)[None]
    y = rng.integers(0, 64, (16, V)); x = s["x"][q, g]; low = np.flatnonzero((dp == 2) | (dp > 3)); x[:, low] = y[:, low]
    x[:, m] = 64 + y[:, m] + 128 * (hi[:, t >> 1] == ((t & 1) == win[t >> 1])[None]).astype(np.int64)
    o = rng.permutation(LA); flip = rng.integers(0, 2, LA)
    return num[LA + 2 * o + flip], num[LA + 2 * o + 1 - flip]
def fold(rng, s, q, g):
    roots = np.concatenate([1 + rng.permutation(R - 1), np.array([0])]); num = R + rng.permutation(V - 1 - R); rows = np.argsort(rng.random((8, 16)), axis=1)[:, :2]
    forced = ([(i >> 1, int(rows[i >> 1, i & 1])) for i in range(16)], [(i, int(rows[i >> 1, i & 1])) for i in range(16)])
    kd, fa, dp = forest(rng, levels(rng.integers(2, 5, C), 8), 3, roots, num, forced)
    s["kd"][q, g], s["fa"][q, g], s["dp"][q, g] = kd, fa, dp
    top = climb(fa, np.arange(V), C); x = s["x"][q, g]; x[:2, np.flatnonzero(top == 0)] = 0; x[2:, 0] = 100
    ln = np.concatenate([np.array([HL, LA - 1]), HL + 1 + rng.permutation(LA - HL - 2)[:6]]); off = (0, 0, 0, 0, 0, 0, -1, 1)
    for i in range(8):
        u = int(roots[i]); goal = (V + off[i] - 977 * int(ln[i])) & (HM - 1); c = kd[:, u]; c = c[c != Z]; c1, c2 = int(num[2 * i]), int(num[2 * i + 1])
        x[:, np.flatnonzero((top == u) & (dp > 0))] = 0
        x[0, c] = goal & 15; x[1, c] = goal >> 4; x[2:, c1] = 100; x[2:6, c2] = 255
        for v, val in ((c1, 200), (c2, 50)):
            t = kd[:, v]; t = t[t != Z]; x[2:, t] = val
    a, b = lanes(rng, fa, dp); apart = np.isin(top[a], np.concatenate([roots[:8], np.array([0])]))
    a = np.where(apart, roots[8 + rng.integers(0, R - 9, LA)], a); a[ln] = roots[:8]; b[ln] = Z
    s["w"][q, g] = 0; s["w"][q, g, 0] = 1; s["w"][q, g, 1] = 16
    return a, b
def setup_inputs_crowd(rng):
    s = base(rng)
    for q in range(N):
        for g in range(8):
            kd, fa = s["kd"][q, g], s["fa"][q, g]; kind = (q + g) % 7; cand = rng.permutation(np.flatnonzero(np.add.reduce((kd != Z).astype(np.int64), axis=0) >= 2))
            if kind < 2:
                P = cand[rng.integers(0, 3, LA)] if kind == 0 else cand[np.arange(LA) % len(cand)]
                o = np.argsort(rng.random((16, LA)) + 2 * (kd[:, P] == Z), axis=0); a, b = kd[o[0], P], kd[o[1], P]
            elif kind == 2:
                a = rng.integers(0, R, LA); b = rng.integers(0, R + 1, LA); b = np.where(b == R, Z, b)
            elif kind == 3:
                a = rng.integers(0, Z, LA); t = rng.integers(0, 4, LA); b = np.where(t < 2, a, np.where(t == 2, climb(fa, a, 1), climb(fa, a, 2)))
            elif kind == 4:
                a, b = pairs(rng, s, q, g)
            elif kind == 5:
                P = rng.permutation(np.unique(fa[R:Z])); P = P[np.arange(LA) % len(P)]
                a = kd[np.argmin(rng.random((16, LA)) + 2 * (kd[:, P] == Z), axis=0), P]; b = a.copy()
            else:
                a, b = fold(rng, s, q, g)
            s["pa"][q, g], s["pb"][q, g] = a, b
    return pack(s)
def check_inputs(d):
    bad = []
    for k, lo, hi in (("xs", 0, 255), ("kd", R, Z), ("fa", 0, Z), ("dp", 0, C), ("pa", 0, Z - 1), ("pb", 0, Z), ("wt", 0, 255)):
        v = np.asarray(d[k]).astype(np.float64)
        if not (np.min(v) >= lo and np.max(v) <= hi): bad.append("range of " + k)
        elif np.any(v != np.floor(v)): bad.append("whole numbers of " + k)
    if bad: return bad
    M = N * 8; f = np.asarray(d["fa"]).astype(np.int64).reshape(M, V); e = np.asarray(d["dp"]).astype(np.int64).reshape(M, V); k = np.asarray(d["kd"]).astype(np.int64).reshape(M, 16 * V)
    if np.any(np.asarray(d["xs"]).astype(np.float32)[..., Z] != 0): bad.append("last column of xs")
    own = np.concatenate([np.arange(R), np.array([Z])])
    if np.any(f[:, own] != own) or np.any(e[:, own] != 0): bad.append("roots")
    if np.any(f[:, R:Z] == Z) or np.any(e[:, R:Z] != np.take_along_axis(e, f[:, R:Z], 1) + 1): bad.append("fathers and depths")
    s = np.sort(k, axis=1)
    if np.any(s[:, :Z - R] != np.arange(R, Z)) or np.any(s[:, Z - R:] != Z): bad.append("every node a kid once")
    if np.any((k != Z) & (np.take_along_axis(f, k, 1) != np.tile(np.arange(V), 16))): bad.append("kids and fathers")
    return bad
def pick(t, ix):
    return np.take_along_axis(t, ix, 1)
def cols(t, ix):
    return np.take_along_axis(t, ix[:, None, :], 2)
def ring(x, k, p, o):
    m = k.shape[0]; K = cols(k, p)
    y = cols(x, K.reshape(m, 16 * LA)).reshape(m, 16, 16, LA)
    score = np.add.reduce(np.maximum(y - cols(x, o)[:, :, None, :], 0), axis=1)
    row = np.argmax(score, axis=1)
    lead = np.take_along_axis(K, row[:, None, :], 1)[:, 0]
    z = cols(x, cols(k, lead).reshape(m, 16 * LA)).reshape(m, 16, 16, LA)
    return K, row, lead, np.max(y, axis=2) + np.max(z, axis=2)
def reference(xs, kd, fa, dp, pa, pb, wt):
    M = N * 8; x = xs.astype(np.float32).astype(np.int32).reshape(M, 16, V); k = kd.astype(np.int64).reshape(M, 16, V); f = fa.astype(np.int64).reshape(M, V); e = dp.astype(np.int64).reshape(M, V)
    a = pa.astype(np.int64).reshape(M, LA); b = pb.astype(np.int64).reshape(M, LA); w = wt.astype(np.int64).reshape(M, 16, 1)
    lane = np.arange(LA); lower = np.tri(LA, k=-1, dtype=bool); at = np.arange(M)[:, None]
    asked = ((at // 8 + 1 + lane[None] % (N - 1)) % N) * 8 + at % 8
    for rnd in range(RO):
        for step in range(C):
            da, db, ga, gb = pick(e, a), pick(e, b), pick(f, a), pick(f, b)
            go = (da != db) | (ga != gb)
            a, b = np.where(go & (da >= db), ga, a), np.where(go & (db >= da), gb, b)
        F = pick(f, a); met = (a != b) & (F == pick(f, b))
        KA, rA, lA, UA = ring(x, k, a, b)
        KB, rB, lB, UB = ring(x, k, b, a)
        awin = met & (np.add.reduce((UA > UB).astype(np.int64), axis=1) >= 9)
        bwin = met & (np.add.reduce((UB > UA).astype(np.int64), axis=1) >= 9)
        first = ~np.any((F[:, :, None] == F[:, None, :]) & lower[None], axis=2)
        W, L = np.where(bwin, b, a), np.where(bwin, a, b); lW, lL = np.where(bwin, lB, lA), np.where(bwin, lA, lB); rW, rL = np.where(bwin, rB, rA), np.where(bwin, rA, rB)
        x2, k2, f2 = x.copy(), k.copy(), f.copy()
        m, i = np.nonzero(first & (awin | bwin))
        x2[m, :, W[m, i]] = (x[m, :, W[m, i]] + x[m, :, lW[m, i]]) >> 1
        m, i = np.nonzero(first & (awin | bwin) & (lW != Z) & (lL != Z))
        k2[m, rW[m, i], W[m, i]] = lL[m, i]; k2[m, rL[m, i], L[m, i]] = lW[m, i]
        f2[m, lW[m, i]] = L[m, i]; f2[m, lL[m, i]] = W[m, i]
        h = np.add.reduce(w * UA, axis=1) & (R - 1)
        m, i = np.nonzero(first & ~met)
        x2[m, :, a[m, i]] = (UA[m, :, i] + 2 * x[asked[m, i], :, h[m, i]]) >> 2
        kid = np.where(bwin[:, None, :], KB, KA)[:, lane & 15, lane]
        new = (np.add.reduce(w * (UA + UB), axis=1) + 977 * lane) & (HM - 1); new = np.where(new >= V, new - V, new)
        a = np.where(lW == Z, W, lW); b = np.where(lane < HL, kid, new)
        x, k, f = x2, k2, f2
    return {"yx": x.reshape(N, 128, V).astype(np.float32).astype(BF), "yf": f.reshape(N, 8, V).astype(np.float32)}

@@ -1,0 +1,664 @@
+from concourse.bass import DstId, RemoteDMATransfer
+from concourse.mybir import AluOpType as OP, ActivationFunctionType as AF
+
+X0, XA, XD, YMO, ZMO, R2O = 896, 2048, 2064, 2320, 2576, 2832
+XEND = R2O + 896
+ND = 4
+
+SCRATCH = {}
+for _n, _w, _d in (
+        ("XW", X0 + XEND, "bfloat16"), ("KD", 2576, "int32"), ("F", 2576, "float32"), ("M", 2048, "bfloat16"), ("VAL", 2048, "bfloat16"), ("CM", 2048, "bfloat16"),
+        ("FAI", 128, "int32"), ("DPI", 128, "int32"), ("PAI", 16, "int32"), ("PBI", 16, "int32"), ("WTI", 1, "int32"), ("FDH", 256, "float16"),
+        ("PI", 1, "int32"), ("TI", 2, "int32"), ("COL", 32, "float32"), ("NF", 256, "float32"), ("NR", 256, "float32"), ("NG", 256, "float32"),
+        ("BLK", 128, "float16"), ("NBLK", 128, "float16"), ("BLK5", 128, "bfloat16"), ("WBH", 144, "float16"), ("WB16", 144, "float16"), ("WBB", 144, "bfloat16"), ("WBW", 144, "bfloat16"),
+        ("IDB", 128, "bfloat16"), ("IDN", 128, "bfloat16"), ("ID2", 128, "bfloat16"), ("IDH", 128, "float16"), ("IDM", 128, "bfloat16"), ("BSEL", 2048, "float16"), ("DELR", 16, "float32"), ("B8", 16, "float32"),
+        ("DM", 256, "bfloat16"), ("RMH", 256, "float16"), ("RMB", 1024, "bfloat16"), ("SEL", 8, "bfloat16"), ("KC", 256, "bfloat16"), ("E0", 128, "bfloat16"), ("ZB", 512, "bfloat16"),
+        ("L15", 16, "uint16"), ("DLT", 128, "float32"), ("E1", 128, "float32"), ("E2", 128, "float32"), ("E3", 128, "float32"), ("P0", 128, "float32"),
+        ("TA", 128, "bfloat16"), ("TB", 128, "bfloat16"), ("DMX", 128, "bfloat16"), ("MS", 128, "bfloat16"), ("RT", 128, "bfloat16"), ("RTN", 128, "bfloat16"), ("RD", 128, "bfloat16"),
+        ("LN", 16, "float32"), ("L977", 16, "float32"), ("QI", 32, "int32"), ("QF", 32, "float32"), ("TBIG", 256, "bfloat16"), ("DUX", 16, "float32"), ("DUF", 32, "float32"),
+        ("BS1", 48, "float32"), ("BS2", 48, "float32"), ("EQ", 2560, "bfloat16"), ("EQS", 2560, "bfloat16"), ("PX", 64, "float32"), ("PT", 64, "float32"), ("PU", 32, "float32"),
+        ("GM", 2560, "bfloat16"), ("G5", 512, "bfloat16"), ("G", 2048, "float16"), ("SC", 2048, "float16"), ("LS", 160, "uint16"), ("LSI", 32, "int32"),
+        ("VA", 256, "float16"), ("PR", 512, "float16"), ("AW", 32, "float32"), ("LA", 32, "uint16"), ("VALF", 512, "float32"),
+        ("KL", 512, "uint16"), ("KF", 512, "float16"), ("XS", 512, "bfloat16"), ("Y", 8192, "bfloat16"), ("SY", 8192, "bfloat16"), ("MM", 8192, "bfloat16"),
+        ("KS", 512, "float32"), ("PS", 512, "float32"), ("OHT", 512, "bfloat16"), ("OHS", 512, "bfloat16"), ("PL", 512, "float16"), ("LL", 32, "uint16"), ("LW", 32, "float32"),
+        ("ZK", 512, "uint16"), ("Z", 8192, "bfloat16"), ("SZ", 8192, "bfloat16"), ("FG", 512, "float16"), ("FW", 32, "float32"), ("FWH", 16, "float16"),
+        ("EQD", 256, "bfloat16"), ("SQD", 256, "bfloat16"), ("GL", 512, "bfloat16"), ("W", 768, "float32"), ("SI", 64, "int32"), ("KDD", 128, "float16"), ("KDS", 128, "float16"), ("KN", 8, "float32"),
+        ("LT", 48, "uint16"), ("LX", 16, "uint16"), ("LF", 64, "uint16"), ("TG", 768, "bfloat16"), ("VI", 256, "int32"), ("TK", 512, "float16"), ("NK", 512, "float32")):
+    SCRATCH[_n] = ("sbuf", [128, _w], _d)
+for _b in range(8):
+    SCRATCH["b%d" % _b] = ("psum", [128, 512], "float32")
+SEMAPHORES = ["qV", "qA", "qT", "qG", "sent1", "sent2", "arr1", "arr2"] + ["d%d" % _i for _i in range(12)]
+
+VY = ((1, 2),)
+RELU = ((1, 0),)
+VG = ((1, 2), (1, 3))
+SLACK = 0.0
+CY, GA, WK = 0.00104, 0.00135, 0.09
+
+
+def X(name, lo, hi, st=1, p0=0, p1=128):
+    return ("x", name, lo, hi, st, p0, p1)
+
+
+def IND(win, off):
+    return ("i", win, off)
+
+
+def width(a):
+    if a[0] == "i":
+        return 16 * (a[2][3] - a[2][2])
+    return (a[3] - a[2] + a[4] - 1) // a[4]
+
+
+def spans(a):
+    return [a[1], a[2]] if a[0] == "i" else [a]
+
+
+def gcd(a, b):
+    while b:
+        a, b = b, a % b
+    return a
+
+
+def clash(a, b):
+    if a[2] >= b[3] or b[2] >= a[3] or a[5] >= b[6] or b[5] >= a[6]:
+        return False
+    return (a[2] - b[2]) % gcd(a[4], b[4]) == 0
+
+
+def two(a):
+    return a[0] == "x" and a[1][0] != "b" and SCRATCH[a[1]][2] in ("bfloat16", "float16", "uint16")
+
+
+def psum(a):
+    return a[0] == "x" and a[1][0] == "b"
+
+
+def build():
+    P = []
+
+    def add(qs, what, out, ins, args, cost, win=None):
+        P.append(dict(q=qs, what=what, out=out, ins=ins, args=args, cost=cost, w=spans(out) if out else [], r=[s for i in ins for s in spans(i)]))
+
+    def ccost(out, ins, fast):
+        n = width(out)
+        if out[0] == "i":
+            return 0.05 + n * 0.0031
+        if ins[0][0] == "i":
+            return 0.05 + n * GA
+        return max(64, n * (0.5 if fast and two(out) and all(two(i) for i in ins) else 1)) * CY
+
+    def tc(out, a, q="V"):
+        add(q, "tc", out, [a], (), ccost(out, [a], True))
+
+    def tt(out, a, b, op):
+        n = width(b)
+        c = 0.05 + n * GA if a[0] == "i" else max(64, n * (1 if psum(a) or psum(b) else 2)) * CY
+        add("V", "tt", out, [a, b], (op,), c)
+
+    def ts(out, a, s1, o1, s2=None, o2=None):
+        ins = [a] + [s for s in (s1, s2) if isinstance(s, tuple)]
+        add("V", "ts", out, ins, (s1, o1, s2, o2), ccost(out, [a], True))
+
+    def scan(out, d0, d1, o0, o1):
+        add("V", "scan", out, [d0, d1], (o0, o1), ccost(out, [d0, d1], True))
+
+    def act(out, a, bias=None):
+        c = 0.065 + width(out) * GA if a[0] == "i" else max(64, width(out)) * CY
+        add("A", "act", out, [a] + ([bias] if bias else []), (bias,), c)
+
+    def relu(out, a):
+        add("A", "relu", out, [a], (), width(out) * CY)
+
+    def gat(out, a, q="A"):
+        add(q, "gat", out, [a], (), 0.06 + width(out) * GA)
+
+    def mm(out, l, r, start, stop):
+        add("T", "mm", out, [l, r], (start, stop), max(64, width(r)) * CY)
+
+    def dma(q, out, a, sem):
+        add(q, "dma", out, [a], (sem,), 0.06)
+
+    def iota(out, pat, cm):
+        add("G", "iota", out, [], (pat, cm), 0.13 + 2 * width(out) * CY)
+
+    def col(i):
+        return X("COL", i, i + 1)
+
+    dma("S", X("FAI", 0, 128), ("d", "fa"), "d0")
+    dma("A", X("DPI", 0, 128), ("d", "dp"), "d1")
+    dma("S", X("PAI", 0, 16), ("d", "pa"), "d2")
+    dma("A", X("PBI", 0, 16), ("d", "pb"), "d3")
+    dma("S", X("KD", 0, 2048), ("d", "kd"), "d5")
+    dma("S", X("XW", X0, X0 + 2048), ("d", "xs"), "d6")
+    dma("S", X("WTI", 0, 1), ("d", "wt"), "d4")
+    add("G", "send", None, [X("XW", X0, X0 + 128)], (1,), 1.0)
+    add("N", "arrive", X("XW", 0, 896), [], (1,), 0)
+
+    iota(X("PI", 0, 1), [[0, 1]], 1)
+    iota(X("NF", 0, 256), [[1, 256]], 0)
+    iota(X("NG", 0, 256), [[1, 16], [0, 16]], 0)
+    iota(X("NR", 0, 256), [[0, 16], [1, 16]], 0)
+    iota(X("XW", X0 + XA, X0 + YMO), [[0, YMO - XA]], 0)
+    iota(X("EQ", 0, 2560), [[0, 2560]], 0)
+    ts(X("TI", 0, 1), X("PI", 0, 1), 15, OP.bitwise_and)
+    ts(X("TI", 1, 2), X("PI", 0, 1), 4, OP.arith_shift_right)
+    tc(X("COL", 0, 2), X("TI", 0, 2))
+    tc(col(2), X("PI", 0, 1))
+    N128, R128, G128 = X("NF", 0, 128), X("NR", 0, 128), X("NG", 0, 128)
+    pr, pg, pc = col(0), col(1), col(2)
+    ts(X("BLK", 0, 128), G128, pg, OP.is_equal)
+    ts(X("DELR", 0, 16), X("NF", 0, 16), pr, OP.is_equal)
+    for r in range(16):
+        ts(X("BSEL", 128 * r, 128 * r + 128), X("BLK", 0, 128), X("DELR", r, r + 1), OP.mult)
+    ts(col(6), pr, 1, OP.is_lt)
+    ts(col(15), pr, 6, OP.is_ge)
+    ts(col(5), pr, 11, OP.is_ge)
+    ts(col(3), pr, 1, OP.is_ge)
+    tt(col(3), col(3), col(15), OP.subtract)
+    tt(col(4), col(15), col(5), OP.subtract)
+    ts(col(7), col(3), 16, OP.mult)
+    ts(col(8), col(5), -4096, OP.mult)
+    ts(col(16), col(4), 5, OP.mult, pr, OP.subtract)
+    ts(col(17), col(5), 10, OP.mult)
+    tt(col(10), col(16), col(17), OP.add)
+    ts(col(18), pr, 1, OP.is_ge, -8192, OP.mult)
+    tc(X("FDH", 0, 128), X("FAI", 0, 128))
+    tc(X("FDH", 128, 256), X("DPI", 0, 128))
+    for k in range(2):
+        for r in range(16):
+            b = "b%d" % (4 * k + r // 4)
+            mm(X(b, 128 * (r % 4), 128 * (r % 4) + 128), X("BSEL", 128 * r, 128 * r + 128), X("FDH", 128 * k, 128 * k + 128), True, True)
+    for i in range(4):
+        act(X("F", 512 * i, 512 * i + 512), X("b%d" % i, 0, 512))
+    add("V", "ms", X("F", XA, XD), [], (2047.0,), 0.066)
+    add("V", "ms", X("KD", XA, XD), [], (2047,), 0.066)
+    ts(X("E1", 0, 128), G128, col(3), OP.mult)
+    ts(X("E2", 0, 128), R128, col(4), OP.mult, col(5), OP.add)
+    tt(X("P0", 0, 128), X("E1", 0, 128), X("E2", 0, 128), OP.add)
+    ts(X("B8", 0, 16), X("NF", 0, 16), 8, OP.mult, col(3), OP.mult)
+    for r in range(16):
+        act(X("VAL", 128 * r, 128 * r + 128), X("P0", 0, 128), X("B8", r, r + 1))
+    ts(X("IDB", 0, 128), N128, pc, OP.is_equal)
+    ts(X("IDM", 0, 128), X("IDB", 0, 128), -256, OP.mult)
+    for i in range(4):
+        add("A", "sq", X("CM", 512 * i, 512 * i + 512), [X("b%d" % (4 + i), 0, 512), col(10)], (), 512 * CY)
+        mm(X("b%d" % i, 0, 512), X("IDB", 0, 128), X("VAL", 512 * i, 512 * i + 512), True, False)
+        mm(X("b%d" % i, 0, 512), X("IDM", 0, 128), X("CM", 512 * i, 512 * i + 512), False, True)
+        relu(X("M", 512 * i, 512 * i + 512), X("b%d" % i, 0, 512))
+    ts(X("TI", 0, 1), X("TI", 1, 2), 1, OP.bitwise_and)
+    tc(col(14), X("TI", 0, 1))
+    ts(col(13), col(14), -1, OP.mult, 1, OP.add)
+    for s in range(2):
+        src = X("PBI" if s else "PAI", 0, 16)
+        ts(X("PX", 32 * s, 32 * s + 16), src, col(13), OP.mult)
+        ts(X("PX", 32 * s + 16, 32 * s + 32), src, col(14), OP.mult)
+    add("V", "tr", X("PT", 0, 64), [X("PX", 0, 64)], (), 0.07)
+    for s in range(2):
+        tt(X("PU", 16 * s, 16 * s + 16), X("PT", 32 * s, 32 * s + 16), X("PT", 32 * s + 16, 32 * s + 32), OP.add)
+    tc(X("LS", 0, 32), X("PU", 0, 32))
+    ts(X("DM", 0, 256), X("NR", 0, 256), pr, OP.is_equal)
+    ts(X("RMH", 0, 256), X("NR", 0, 256), 0, OP.not_equal)
+    ts(X("DLT", 0, 128), R128, pr, OP.subtract)
+    ts(X("E3", 0, 128), R128, 5, OP.is_le)
+    tt(X("BLK5", 0, 128), X("E3", 0, 128), X("BLK", 0, 128), OP.mult)
+    b5, dl, e1, e2, e3 = X("BLK5", 0, 128), X("DLT", 0, 128), X("E1", 0, 128), X("E2", 0, 128), X("E3", 0, 128)
+    m128 = lambda n: X(n, 0, 128)
+    ts(e1, dl, 1, OP.is_equal, col(7), OP.mult)
+    ts(e2, dl, -4, OP.is_equal, col(4), OP.mult)
+    tt(e3, e1, e2, OP.add)
+    tt(m128("TA"), e3, b5, OP.mult)
+    ts(m128("TB"), m128("TA"), -1, OP.mult)
+    ts(e1, dl, -10, OP.is_le, col(8), OP.mult)
+    ts(e2, R128, 1, OP.is_ge)
+    tt(e3, e1, e2, OP.mult)
+    tt(m128("MS"), e3, b5, OP.mult)
+    ts(e1, dl, 0, OP.is_equal, col(7), OP.mult)
+    ts(e2, dl, -5, OP.is_equal, col(4), OP.mult)
+    tt(e3, e1, e2, OP.add)
+    tt(e1, e3, b5, OP.mult)
+    tt(m128("DMX"), e1, m128("TA"), OP.subtract)
+    ts(e1, dl, 1, OP.is_equal, col(6), OP.mult)
+    tt(m128("RT"), e1, b5, OP.mult)
+    ts(m128("RTN"), m128("RT"), -1, OP.mult)
+    ts(e1, dl, 0, OP.is_equal, col(6), OP.mult)
+    tt(e2, e1, b5, OP.mult)
+    tt(m128("RD"), e2, m128("RT"), OP.subtract)
+    add("V", "ms", X("ZB", 0, 512), [], (0.0,), 0.27)
+    ts(X("WBH", 0, 144), X("NF", 0, 144), 0, OP.mult)
+    ts(X("WBH", 15, 143, 16), X("NF", 0, 8), pg, OP.is_equal)
+    ts(X("WB16", 0, 144), X("WBH", 0, 144), 0.0625, OP.mult)
+    tc(X("WBB", 0, 144), X("WBH", 0, 144))
+    tc(col(12), X("WTI", 0, 1))
+    ts(X("WBW", 0, 144), X("WBB", 0, 144), col(12), OP.mult)
+    ts(m128("NBLK"), m128("BLK"), -1, OP.mult)
+    ts(m128("IDN"), m128("IDB"), -1, OP.mult)
+    ts(m128("ID2"), m128("IDB"), 2, OP.mult)
+    tc(m128("IDH"), m128("IDB"))
+    tc(X("RMB", 0, 256), X("RMH", 0, 256))
+    tc(X("RMB", 256, 512), X("RMB", 0, 256))
+    tc(X("RMB", 512, 1024), X("RMB", 0, 512))
+    ts(X("SEL", 0, 8), X("NF", 0, 8), pg, OP.is_equal, 16, OP.mult)
+    ts(X("KC", 0, 256), X("NR", 0, 256), -1, OP.mult, 15, OP.add)
+    ts(col(11), pc, 0, OP.is_equal)
+    ts(m128("E0"), N128, 0, OP.mult, col(11), OP.add)
+    ts(X("L15", 0, 16), X("NF", 0, 16), 16, OP.mult, 15, OP.add)
+    n16 = X("NF", 0, 16)
+    ts(X("LN", 0, 16), n16, 16, OP.mult, pr, OP.add)
+    ln = X("LN", 0, 16)
+    ts(X("L977", 0, 16), ln, 977, OP.mult)
+    ts(X("QI", 0, 16), ln, 9363, OP.mult)
+    ts(X("QI", 16, 32), X("QI", 0, 16), 16, OP.arith_shift_right)
+    ts(X("QF", 0, 16), X("QI", 16, 32), -7, OP.mult)
+    tt(X("QF", 16, 32), X("QF", 0, 16), ln, OP.add)
+    for nm, base in (("BS1", -896), ("BS2", R2O)):
+        ts(X(nm, 0, 16), ln, YMO, OP.add)
+        ts(X(nm, 16, 32), ln, ZMO, OP.add)
+        ts(X(nm, 32, 48), X("QF", 16, 32), 128, OP.mult, base, OP.add)
+    ts(X("TBIG", 0, 256), X("NR", 0, 256), pr, OP.is_ge, 4096, OP.mult)
+    ts(X("DUX", 0, 16), ln, XD, OP.add)
+    ts(X("DUF", 0, 16), ln, XD, OP.add)
+    ts(X("DUF", 16, 32), ln, XD + 256, OP.add)
+
+    xwin, kwin, fwin, mwin = X("XW", X0, X0 + XD), X("KD", 0, XD), X("F", 0, XD), X("M", 0, 2048)
+    for rnd in range(2):
+        last = rnd == 1
+        mm(X("b1", 0, 512), m128("IDB"), X("ZB", 0, 512), True, False)
+        for k in range(5):
+            for s in range(2):
+                ls = X("LS", 32 * k + 16 * s, 32 * k + 16 * s + 16)
+                o = 256 * s
+                if k < 4:
+                    g = X("G", 512 * k + o, 512 * k + o + 256)
+                    sc = ("SC", 512 * k + o, 512 * k + o + 256)
+                    tt(g, IND(X("F", 0, 2048), ls), X("DM", 0, 256), OP.mult)
+                    scan(X(*sc), X("RMH", 0, 256), g, OP.mult, OP.add)
+                    tc(X("LS", 32 * k + 32 + 16 * s, 32 * k + 48 + 16 * s), X(sc[0], sc[1] + 15, sc[2], 16))
+                gm = X("GM", 512 * k + o, 512 * k + o + 256)
+                gat(gm, IND(mwin, ls))
+                if k == 4:
+                    g5 = X("G5", o, o + 256)
+                    add("V", "tc", g5, [IND(X("F", 0, 2048), ls)], (), 0.05 + 256 * GA)
+                mm(X("b0", 0, 256), m128("TB" if s else "TA"), gm, k == 0 and s == 0, k == 4 and s == 1 and False)
+                if k == 0:
+                    mm(X("b0", 0, 256), m128("MS"), gm, False, False)
+                mm(X("b1", o, o + 256), m128("DMX"), gm, False, False)
+                if k == 4:
+                    mm(X("b0", 0, 256), m128("RTN" if s else "RT"), g5, False, s == 1)
+                    mm(X("b1", o, o + 256), m128("RD"), g5, False, s == 1)
+        ts(X("VA", 0, 256), X("b0", 0, 256), col(18), OP.is_equal)
+        for s in range(2):
+            tt(X("PR", 256 * s, 256 * s + 256), X("b1", 256 * s, 256 * s + 256), X("VA", 0, 256), OP.mult)
+        for r in range(16):
+            mm(X("b2", 0, 32), X("WBH", 15 - r, 143 - r), X("PR", r, 512, 16), r == 0, r == 15)
+        tc(X("LA", 0, 32), X("b2", 0, 32))
+        tc(X("AW", 0, 32), X("b2", 0, 32))
+        mm(X("b3", 0, 512), m128("BLK"), X("PR", 0, 512), True, True)
+        act(X("VALF", 256, 512), X("b3", 0, 256))
+        act(X("VALF", 0, 256), X("b3", 256, 512))
+
+        def la(s):
+            return X("LA", 16 * s, 16 * s + 16)
+        for s in range(2):
+            gat(X("XS", 256 * s, 256 * s + 256), IND(xwin, la(s)))
+            mm(X("b4", 256 - 256 * s, 512 - 256 * s), m128("IDB"), X("XS", 256 * s, 256 * s + 256), True, True)
+        for s in range(2):
+            tc(X("KL", 256 * s, 256 * s + 256), IND(kwin, la(s)))
+        for s in range(2):
+            for q in range(4):
+                gat(X("Y", 4096 * s + 1024 * q, 4096 * s + 1024 * q + 1024), IND(xwin, X("KL", 256 * s + 64 * q, 256 * s + 64 * q + 64)), "V" if (s, q) in VY else "A")
+        for s in range(2):
+            tc(X("KF", 256 * s, 256 * s + 256), X("KL", 256 * s, 256 * s + 256))
+        for s in range(2):
+            kb = "b%d" % (5 + s)
+            mm(X(kb, 0, 256), m128("E0"), X("KC", 0, 256), True, False)
+            for h in range(2):
+                base = 4096 * s + 2048 * h
+                for i in range(4):
+                    for j in range(4 * i, 4 * i + 4):
+                        y, m = X("Y", base + j, base + 2048, 16), X("MM", base + 128 * j, base + 128 * j + 128)
+                        if (s, h) in RELU:
+                            b = "b%d" % (i % 2)
+                            c = 128 * (j - 4 * i)
+                            mm(X(b, c, c + 128), m128("IDB"), y, True, False)
+                            mm(X(b, c, c + 128), m128("IDN"), X("XS", 256 - 256 * s + 128 * h, 384 - 256 * s + 128 * h), False, True)
+                        else:
+                            tt(m, y, X("b4", 256 * s + 128 * h, 256 * s + 128 * h + 128), OP.max)
+                    if (s, h) in RELU:
+                        relu(X("MM", base + 512 * i, base + 512 * i + 512), X("b%d" % (i % 2), 0, 512))
+                    for j in range(4 * i, 4 * i + 4):
+                        mm(X(kb, 128 * h + j, 128 * h + 128, 16), X("MM", base + 128 * j, base + 128 * j + 128), X("SEL", 0, 8), False, h == 1 and j == 15)
+        for s in range(2):
+            o = 256 * s
+            kb = "b%d" % (5 + s)
+            tc(X("KS", o, o + 256), X(kb, 0, 256))
+            scan(X("PS", o, o + 256), X("RMH", 0, 256), X("KS", o, o + 256), OP.mult, OP.max)
+            tt(X("OHT", o, o + 256), IND(X("PS", o, o + 256), X("L15", 0, 16)), X("KS", o, o + 256), OP.is_equal)
+            for h in range(2):
+                mm(X("b7", o + 128 * h, o + 128 * h + 128), X("OHT", o + 128 * h, o + 128 * h + 128), m128("IDB"), True, True)
+            tt(X("PL", o, o + 256), X("b7", o, o + 256), X("KF", o, o + 256), OP.mult)
+            for r in range(16):
+                mm(X("b3", 16 * s, 16 * s + 16), X("WBH", 15 - r, 143 - r), X("PL", o + r, o + 256, 16), r == 0, r == 15)
+            tc(X("LL", 16 * s, 16 * s + 16), X("b3", 16 * s, 16 * s + 16))
+            tc(X("LW", 16 * s, 16 * s + 16), X("b3", 16 * s, 16 * s + 16))
+            tc(X("ZK", o, o + 256), IND(kwin, X("LL", 16 * s, 16 * s + 16)))
+            for q in range(4):
+                gat(X("Z", 4096 * s + 1024 * q, 4096 * s + 1024 * q + 1024), IND(xwin, X("ZK", o + 64 * q, o + 64 * q + 64)), "AV" if (s, q) in VG else "A")
+            if not last:
+                act(X("OHS", o, o + 256), X("b7", o, o + 256))
+        for n1, n2 in (("Y", "SY"), ("Z", "SZ")):
+            for s in range(2):
+                for q in range(4):
+                    lo = 4096 * s + 1024 * q
+                    scan(X(n2, lo, lo + 1024), X("RMB", 0, 1024), X(n1, lo, lo + 1024), OP.mult, OP.max)
+        for s in range(2):
+            tc(X("FG", 256 * s, 256 * s + 256), IND(fwin, la(s)))
+        for r in range(16):
+            mm(X("b2", 0, 32), X("WB16", 15 - r, 143 - r), X("FG", r, 512, 16), r == 0, r == 15)
+        tc(X("FW", 0, 32), X("b2", 0, 32))
+        tc(X("FWH", 0, 16), X("FW", 0, 16))
+        mm(X("b2", 0, 256), m128("IDB"), X("TBIG", 0, 256), True, False)
+        for r in range(16):
+            mm(X("b2", r, 256, 16), m128("IDH"), X("FWH", 0, 16), False, r == 15)
+        tt(X("EQD", 0, 256), X("FG", 0, 256), X("b2", 0, 256), OP.is_equal)
+        scan(X("SQD", 0, 256), X("RMH", 0, 256), X("EQD", 0, 256), OP.mult, OP.max)
+        for c in range(1, 16):
+            k = c // 4
+            o = 128 * k * (k + 1) + (c - 4 * k) * 64 * (k + 1)
+            ts(X("EQ", o, o + 16 * c), X("FG", 0, 16 * c), X("FW", c, c + 1), OP.is_equal, c + 1, OP.mult)
+        scan(X("EQS", 0, 2560), X("EQ", 0, 2560), X("EQ", 0, 2560), OP.max, OP.max)
+
+        def w(i, n=1):
+            return X("W", 16 * i, 16 * (i + n))
+        for k in range(4):
+            b = 128 * k * (k + 1)
+            n = 64 * (k + 1)
+            tt(X("W", 4 * k, 4 * k + 4), X("EQS", b + n - 1, b + 4 * n, n), X("NF", 1 + 4 * k, 5 + 4 * k), OP.not_equal)
+        ts(w(1), X("SQD", 15, 256, 16), 0, OP.is_equal)
+        tt(w(2), w(0), w(1), OP.mult)
+        tt(w(3), X("AW", 0, 16), X("AW", 16, 32), OP.not_equal)
+        tt(w(4), X("FW", 0, 16), X("FW", 16, 32), OP.is_equal)
+        tt(w(5), w(3), w(4), OP.mult)
+        tt(w(6), w(2), w(5), OP.mult)
+        tt(w(7), w(2), w(6), OP.subtract)
+        ts(w(12, 2), X("LW", 0, 32), 2047, OP.not_equal)
+        tt(w(14), w(12), w(13), OP.mult)
+        tt(w(15), w(14), w(6), OP.mult)
+        tc(w(8), X("AW", 0, 16))
+        tc(w(9), X("LW", 0, 16))
+        tt(w(10), X("AW", 16, 32), X("AW", 0, 16), OP.subtract)
+        tt(w(11), X("LW", 16, 32), X("LW", 0, 16), OP.subtract)
+        tt(w(16, 2), X("LW", 0, 32), X("DUF", 0, 32), OP.subtract)
+        if not last:
+            tt(w(18, 2), X("AW", 0, 32), X("DUF", 0, 32), OP.subtract)
+        for i, src in enumerate(("SY", "SZ")):
+            for r in range(16):
+                mm(X("b5", 0, 32), X("WBW", 15 - r, 143 - r), X(src, 15 + 16 * r, 8192, 256), i == 0 and r == 0, i == 1 and r == 15)
+        tc(X("XW", X0 + YMO, X0 + YMO + 256), X("SY", 15, 4096, 16))
+        tc(X("XW", X0 + ZMO, X0 + ZMO + 256), X("SZ", 15, 4096, 16))
+        for i, src in enumerate(("SY", "SZ")):
+            for s in range(2):
+                mm(X("b6", 0, 256), m128("IDN" if s else "IDB"), X(src, 4096 * s + 15, 4096 * s + 4096, 16), i + s == 0, i + s == 2)
+        ts(X("GL", 0, 256), X("b6", 0, 256), 0, OP.is_gt)
+        ts(X("GL", 256, 512), X("b6", 0, 256), 0, OP.is_lt)
+        for r in range(16):
+            mm(X("b2", 0, 32), X("WBB", 15 - r, 143 - r), X("GL", r, 512, 16), r == 0, r == 15)
+        tc(X("SI", 0, 32), X("b5", 0, 32))
+        bs = "BS2" if last else "BS1"
+        ts(X("SI", 32, 48), X("SI", 0, 16), 127, OP.bitwise_and)
+        tt(w(24), X("SI", 32, 48), X(bs, 32, 48), OP.add)
+        tc(w(22, 2), X(bs, 0, 32))
+        ts(w(20, 2), X("b2", 0, 32), 9, OP.is_ge)
+        tt(w(25), w(20), w(21), OP.add)
+        tt(w(26), w(21), w(5), OP.mult)
+        tt(w(27), w(21), w(5), OP.mult)
+        tt(w(30), w(25), w(15), OP.mult)
+        tt(w(28, 2), w(26, 2), w(10, 2), OP.mult)
+        tt(w(31), w(25), w(15), OP.mult)
+        tt(w(32, 2), w(28, 2), w(8, 2), OP.add)
+        tt(w(34, 2), w(30, 2), w(16, 2), OP.mult)
+        tt(w(36, 2), w(34, 2), X("DUF", 0, 32), OP.add)
+        tc(X("LF", 0, 32), w(36, 2))
+        add("V", "tc", IND(X("F", 0, 2576), X("LF", 0, 32)), [X("VALF", 0, 512)], (), 0.05 + 512 * 0.0031)
+        for i in range(3):
+            tt(w(38 + i), w(25), w(5), OP.mult)
+        for i in range(3):
+            tt(w(41 + i), w(33 if i == 2 else 32), w(22 + i), OP.subtract)
+        tt(X("W", 704, 752), X("W", 608, 656), X("W", 656, 704), OP.mult)
+        tt(X("W", 656, 704), X("W", 704, 752), X("W", 352, 400), OP.add)
+        ts(X("LT", 0, 48), X("W", 656, 704), 0 if last else X0, OP.add)
+        twin = X("XW", X0, X0 + XEND) if last else X("XW", 0, X0 + R2O)
+        for i in range(3):
+            gat(X("TG", 256 * i, 256 * i + 256), IND(twin, X("LT", 16 * i, 16 * i + 16)), "AV")
+        for i in range(3):
+            mm(X("b3", 0, 256), m128("ID2" if i == 2 else "IDB"), X("TG", 256 * i, 256 * i + 256), i == 0, i == 2)
+        tt(w(28), w(6), w(25), OP.mult)
+        tt(w(29), w(28), w(7), OP.add)
+        tt(w(28), w(32), X("DUX", 0, 16), OP.subtract)
+        tt(w(34), w(28), w(29), OP.mult)
+        tt(w(35), w(34), X("DUX", 0, 16), OP.add)
+        tc(X("LX", 0, 16), w(35))
+        ts(X("VI", 0, 256), X("b3", 0, 256), 0.25, OP.mult, -0.375, OP.add)
+        add("W", "waitsent", X("XW", X0, X0 + 128), [], (rnd + 1,), 0)
+        add("V", "tc", IND(X("XW", X0, X0 + YMO), X("LX", 0, 16)), [X("VI", 0, 256)], (), 0.05 + 256 * 0.0031)
+        if last:
+            dma("S", ("d", "yf"), X("F", 0, 2048, 1, 0, 128), "d7")
+            for i in range(2):
+                dma("SA"[i], ("d", "yx%d" % i), X("XW", X0 + 1024 * i, X0 + 1024 * i + 1024), "d%d" % (8 + i))
+            break
+        add("G", "send", None, [X("XW", X0, X0 + 128)], (2,), 1.0)
+        add("N", "arrive", X("XW", X0 + R2O, X0 + XEND), [], (2,), 0)
+        ts(w(28), w(33), 2047, OP.is_equal)
+        tt(w(29), w(32), w(33), OP.subtract)
+        tt(w(34), w(28), w(29), OP.mult)
+        tt(w(35), w(34), w(33), OP.add)
+        tc(X("LS", 0, 16), w(35))
+        for s in range(2):
+            tt(X("KDD", 64 * s, 64 * s + 64), X("KF", 256 * s, 256 * s + 64), X("DM", 0, 64), OP.mult)
+        scan(X("KDS", 0, 128), X("RMH", 0, 128), X("KDD", 0, 128), OP.mult, OP.add)
+        tc(X("KN", 0, 8), X("KDS", 15, 128, 16))
+        tt(X("W", 704, 708), X("KN", 4, 8), X("KN", 0, 4), OP.subtract)
+        tt(X("W", 708, 712), X("W", 704, 708), X("W", 416, 420), OP.mult)
+        tt(X("LSI", 0, 4), X("W", 708, 712), X("KN", 0, 4), OP.add)
+        tt(X("SI", 48, 64), X("SI", 0, 16), X("SI", 16, 32), OP.add)
+        tt(X("LSI", 16, 32), X("SI", 48, 64), X("L977", 0, 16), OP.add)
+        ts(X("LSI", 4, 16), X("LSI", 20, 32), 2047, OP.bitwise_and)
+        tc(X("LS", 16, 32), X("LSI", 0, 16))
+        mm(X("b1", 0, 256), m128("BLK"), X("PL", 256, 512), True, False)
+        mm(X("b1", 0, 256), m128("NBLK"), X("PL", 0, 256), False, True)
+        tt(X("TK", 0, 256), X("b1", 0, 256), X("OHS", 0, 256), OP.mult)
+        ts(X("OHS", 256, 512), X("OHS", 256, 512), -1, OP.mult)
+        tt(X("TK", 256, 512), X("b1", 0, 256), X("OHS", 256, 512), OP.mult)
+        mm(X("b4", 0, 512), m128("IDH"), X("TK", 0, 512), True, False)
+        mm(X("b4", 0, 512), m128("IDH"), X("KF", 0, 512), False, True)
+        act(X("NK", 0, 512), X("b4", 0, 512))
+        tt(w(34, 2), w(30, 2), w(18, 2), OP.mult)
+        tt(w(36, 2), w(34, 2), X("DUF", 0, 32), OP.add)
+        tc(X("LF", 32, 64), w(36, 2))
+        add("V", "tc", IND(X("KD", 0, 2576), X("LF", 32, 64)), [X("NK", 0, 512)], (), 0.05 + 512 * 0.0031)
+    return P
+
+
+def deps(P):
+    hist, n = {}, len(P)
+    preds = [dict() for _ in P]
+    for i, p in enumerate(P):
+        for acc, wr in [(a, False) for a in p["r"]] + [(a, True) for a in p["w"]]:
+            if acc[0] != "x":
+                continue
+            L = hist.setdefault(acc[1], [])
+            for j, b, bw in L:
+                if j == i:
+                    continue
+                if acc[1][0] == "b":
+                    both = p["q"] == "T" and P[j]["q"] == "T"
+                    if p["q"] != P[j]["q"] or ((wr or bw) and clash(acc, b) and not both):
+                        preds[i][j] = True
+                    else:
+                        preds[i].setdefault(j, False)
+                elif (wr or bw) and clash(acc, b):
+                    preds[i][j] = True
+            L.append((i, acc, wr))
+    return preds
+
+
+def order(P, preds):
+    n = len(P)
+    succ = [[] for _ in P]
+    for i in range(n):
+        for j in preds[i]:
+            succ[j].append(i)
+    prio = [0.0] * n
+    for i in range(n - 1, -1, -1):
+        lat = 2.0 if P[i]["what"] == "dma" else 0.0
+        prio[i] = P[i]["cost"] + lat + max([prio[k] + WK for k in succ[i]] + [0.0])
+    left = [len(p) for p in preds]
+    ready = {i: 0.0 for i in range(n) if not left[i]}
+    free = {q: 0.0 for q in "AVTGSNW"}
+    seq, queue = [], [None] * n
+    while ready:
+        cand = []
+        for i, t in ready.items():
+            qs = P[i]["q"]
+            q = min(qs, key=lambda z: max(free[z], t)) if len(qs) > 1 else qs
+            cand.append((max(free[q], t), -prio[i], i, q))
+        first = min(cand)
+        st, _, i, q = min((c for c in cand if c[3] == first[3] and c[0] <= first[0] + SLACK), key=lambda c: (c[1], c[0]))
+        queue[i] = q
+        end = st + P[i]["cost"]
+        free[q] = end
+        if P[i]["what"] == "dma":
+            end += 2.0
+        if P[i]["what"] == "arrive":
+            end += 12.0
+        P[i]["t"] = (st, end)
+        seq.append(i)
+        del ready[i]
+        for k in succ[i]:
+            left[k] -= 1
+            if not left[k]:
+                ready[k] = max([P[j]["t"][1] + (WK if preds[k][j] else 0.0) for j in preds[k]])
+    return seq, queue, preds
+
+
+PLAN = {}
+
+
+def plan():
+    if not PLAN:
+        P = build()
+        preds = deps(P)
+        PLAN["p"] = (P,) + order(P, preds)
+    return PLAN["p"]
+
+
+def rank_program(g, core, T, topo):
+    rank = T.rank_of(core)
+    if rank is None:
+        return
+    P, seq, queue, preds = plan()
+    eng = {"V": g.vector, "A": g.scalar, "T": g.tensor, "G": g, "S": g.sync}
+    cores = list(T.cores)
+    n = len(cores)
+
+    def ap(a):
+        if a[0] == "i":
+            return ap(a[1]).indirect(ap(a[2]))
+        if a[0] == "d":
+            if a[1] == "yf":
+                return T.yf[:]
+            if a[1][:2] == "yx":
+                i = int(a[1][2:])
+                return T.yx[:, 1024 * i:1024 * i + 1024]
+            return T[a[1]][:]
+        _, name, lo, hi, st, p0, p1 = a
+        return T[name][p0:p1, lo:hi] if st == 1 else T[name][p0:p1, lo:hi:st]
+
+    def sc(s):
+        return ap(s) if isinstance(s, tuple) else s
+
+    count = {"V": 0, "A": 0, "T": 0, "G": 0}
+    done, total = {}, {}
+    seen = {q: {} for q in "VATGS"}
+
+    def wait(q, sem, v):
+        if seen[q].get(sem, 0) < v:
+            seen[q][sem] = v
+            eng[q].wait_ge(T.sem[sem], v)
+
+    extra = {}
+    for i in seq:
+        p, q = P[i], queue[i]
+        what, args = p["what"], p["args"]
+        if what == "arrive":
+            done[i] = [("arr%d" % args[0], ND * (n - 1))]
+            total["arr%d" % args[0]] = ND * (n - 1)
+            continue
+        if what == "waitsent":
+            done[i] = [s for j in preds[i] for s in done[j]] + [("sent%d" % args[0], ND)]
+            continue
+        need = {}
+        for j, hard in preds[i].items():
+            if hard:
+                for sem, v in done[j]:
+                    need[sem] = max(need.get(sem, 0), v)
+        for sem in sorted(need):
+            wait(q, sem, need[sem])
+        out = p["out"] and ap(p["out"])
+        ins = [ap(a) for a in p["ins"]]
+        e = eng[q]
+        if what == "dma":
+            src = ins[0]
+            if p["out"][1] == "yf":
+                src = T.F[0::16, 0:2048]
+            e.dma_start(out, src).then_inc(T.sem[args[0]], 16)
+            done[i] = [(args[0], 16)]
+            total[args[0]] = 16
+            continue
+        if what == "send":
+            base = (0 if args[0] == 1 else X0 + R2O)
+            others = [cores[(rank + d) % n] for d in range(1, n)]
+            engines = [x for x in topo.engines(core, others[0]) if all(x in topo.engines(core, o) for o in others)][:ND]
+            ids, dsts = [], []
+            for o in others:
+                rid, pid, _s = topo.addr(o)
+                slot = (rank - T.rank_of(o) - 1) % n
+                ids.append(DstId(rid=rid, pnc=pid))
+                dsts.append(T.XW[:, base + 128 * slot:base + 128 * slot + 128])
+            g.remote_dma_fused([RemoteDMATransfer(dst_ids=ids, dma_engine_mask=sum(1 << x for x in engines), remote_sem=T.sem["arr%d" % args[0]], srcs=[ins[0]], dsts=dsts)], local_sem=T.sem["sent%d" % args[0]])
+            done[i] = [("sent%d" % args[0], ND)]
+            total["sent%d" % args[0]] = ND
+            continue
+        if what == "tc" or (what == "gat" and q == "V"):
+            h = e.tensor_copy(out, ins[0])
+        elif what == "gat":
+            h = e.activation(out, ins[0], AF.Copy)
+        elif what == "sq":
+            h = e.activation(out, ins[0], AF.Square, bias=ins[1])
+        elif what == "relu":
+            h = e.activation(out, ins[0], AF.Relu)
+        elif what == "act":
+            h = e.activation(out, ins[0], AF.Identity, bias=ins[1]) if args[0] else e.activation(out, ins[0], AF.Copy)
+        elif what == "tt":
+            h = e.tensor_tensor(out, ins[0], ins[1], args[0])
+        elif what == "ts":
+            s1, o1, s2, o2 = args
+            h = e.tensor_scalar(out, ins[0], sc(s1), None, o1) if o2 is None else e.tensor_scalar(out, ins[0], sc(s1), sc(s2), o1, o2)
+        elif what == "scan":
+            h = e.tensor_tensor_scan(out, ins[0], ins[1], 0.0, args[0], args[1])
+        elif what == "mm":
+            h = e.matmul(out, ins[0], ins[1], args[0], args[1])
+        elif what == "tr":
+            h = e.transpose(out, ins[0])
+        elif what == "ms":
+            h = e.memset(out, args[0])
+        elif what == "iota":
+            h = e.iota(out, args[0], 0, args[1], allow_small_or_imprecise_dtypes=True)
+        h.then_inc(T.sem["q" + q], 1)
+        count[q] += 1
+        done[i] = [("q" + q, count[q])]
+    for q in "VATG":
+        if count[q]:
+            wait("S", "q" + q, count[q])
+    for sem in sorted(total):
+        wait("S", sem, total[sem])

@@ -10,29 +10,32 @@ for _n, _w, _d in (
         ("XW", X0 + XEND, "bfloat16"), ("KD", 2576, "int32"), ("F", 2576, "float32"), ("M", 2048, "bfloat16"), ("VAL", 2048, "bfloat16"), ("CM", 2048, "bfloat16"),
         ("FAI", 128, "int32"), ("DPI", 128, "int32"), ("PAI", 16, "int32"), ("PBI", 16, "int32"), ("WTI", 1, "int32"), ("FDH", 256, "float16"),
         ("PI", 1, "int32"), ("TI", 2, "int32"), ("COL", 32, "float32"), ("NF", 256, "float32"), ("NR", 256, "float32"), ("NG", 256, "float32"),
-        ("BLK", 128, "float16"), ("NBLK", 128, "float16"), ("BLK5", 128, "bfloat16"), ("WBH", 144, "float16"), ("WB16", 144, "float16"), ("WBB", 144, "bfloat16"), ("WBW", 144, "bfloat16"),
+        ("BLK", 128, "float16"), ("NBLK", 128, "float16"), ("WBH", 144, "float16"), ("WB16", 144, "float16"), ("WBB", 144, "bfloat16"), ("WBW", 144, "bfloat16"),
         ("IDB", 128, "bfloat16"), ("IDN", 128, "bfloat16"), ("ID2", 128, "bfloat16"), ("IDH", 128, "float16"), ("IDM", 128, "bfloat16"), ("BSEL", 2048, "float16"), ("DELR", 16, "float32"), ("B8", 16, "float32"),
         ("DM", 256, "bfloat16"), ("RMH", 256, "float16"), ("RMB", 1024, "bfloat16"), ("SEL", 8, "bfloat16"), ("KC", 256, "bfloat16"), ("E0", 128, "bfloat16"), ("ZB", 512, "bfloat16"),
-        ("L15", 16, "uint16"), ("DLT", 128, "float32"), ("E1", 128, "float32"), ("E2", 128, "float32"), ("E3", 128, "float32"), ("P0", 128, "float32"),
+        ("L15", 16, "uint16"), ("DLT", 128, "bfloat16"), ("S1", 128, "bfloat16"), ("S2", 128, "bfloat16"), ("S3", 128, "bfloat16"), ("S4", 128, "bfloat16"), ("S5", 128, "bfloat16"), ("S6", 256, "bfloat16"), ("E4", 256, "float32"), ("E1", 128, "float32"), ("E2", 128, "float32"), ("E3", 128, "float32"), ("P0", 128, "float32"),
         ("TA", 128, "bfloat16"), ("TB", 128, "bfloat16"), ("DMX", 128, "bfloat16"), ("MS", 128, "bfloat16"), ("RT", 128, "bfloat16"), ("RTN", 128, "bfloat16"), ("RD", 128, "bfloat16"),
         ("LN", 16, "float32"), ("L977", 16, "float32"), ("QI", 32, "int32"), ("QF", 32, "float32"), ("TBIG", 256, "bfloat16"), ("DUX", 16, "float32"), ("DUF", 32, "float32"),
-        ("BS1", 48, "float32"), ("BS2", 48, "float32"), ("EQ", 2560, "bfloat16"), ("EQS", 2560, "bfloat16"), ("PX", 64, "float32"), ("PT", 64, "float32"), ("PU", 32, "float32"),
+        ("RBK", 32, "float32"), ("CNT", 16, "float32"), ("BS1", 48, "float32"), ("BS2", 48, "float32"), ("EQ", 2560, "bfloat16"), ("EQS", 2560, "bfloat16"), ("PX", 64, "float32"), ("PT", 64, "float32"), ("PU", 32, "float32"),
         ("GM", 2560, "bfloat16"), ("G5", 512, "bfloat16"), ("G", 2048, "float16"), ("SC", 2048, "float16"), ("LS", 160, "uint16"), ("LSI", 32, "int32"),
         ("VA", 256, "float16"), ("PR", 512, "float16"), ("AW", 32, "float32"), ("LA", 32, "uint16"), ("VALF", 512, "float32"),
         ("KL", 512, "uint16"), ("KF", 512, "float16"), ("XS", 512, "bfloat16"), ("Y", 8192, "bfloat16"), ("SY", 8192, "bfloat16"), ("MM", 8192, "bfloat16"),
         ("KS", 512, "float32"), ("PS", 512, "float32"), ("OHT", 512, "bfloat16"), ("OHS", 512, "bfloat16"), ("PL", 512, "float16"), ("LL", 32, "uint16"), ("LW", 32, "float32"),
         ("ZK", 512, "uint16"), ("Z", 8192, "bfloat16"), ("SZ", 8192, "bfloat16"), ("FG", 512, "float16"), ("FW", 32, "float32"), ("FWH", 16, "float16"),
-        ("EQD", 256, "bfloat16"), ("SQD", 256, "bfloat16"), ("GL", 512, "bfloat16"), ("W", 768, "float32"), ("SI", 64, "int32"), ("KDD", 128, "float16"), ("KDS", 128, "float16"), ("KN", 8, "float32"),
+        ("EQD", 256, "bfloat16"), ("SQD", 256, "bfloat16"), ("GL", 512, "bfloat16"), ("W", 1152, "float32"), ("SI", 64, "int32"), ("KDD", 128, "float16"), ("KDS", 128, "float16"), ("KN", 8, "float32"),
         ("LT", 48, "uint16"), ("LX", 16, "uint16"), ("LF", 64, "uint16"), ("TG", 768, "bfloat16"), ("VI", 256, "int32"), ("TK", 512, "float16"), ("NK", 512, "float32")):
     SCRATCH[_n] = ("sbuf", [128, _w], _d)
 for _b in range(8):
     SCRATCH["b%d" % _b] = ("psum", [128, 512], "float32")
 SEMAPHORES = ["qV", "qA", "qT", "qG", "sent1", "sent2", "arr1", "arr2"] + ["d%d" % _i for _i in range(12)]
 
-VY = ((1, 2),)
+VY = ((1, 0),)
 RELU = ((1, 0),)
-VG = ((1, 2), (1, 3))
+VG = ((0, 0), (1, 1), (1, 3))
 SLACK = 0.0
+KSA, FQ, MQ, GQ = "VA", "VAAV", "AAVA", "AAAAAAAAVA"
+BOOST = {"ma": 6.0, "la": 20.0, "lb": -2.0, "SZ": 32.0, "zb": -4.0, "za": -4.0}
+G5Q = "AAAA"
 CY, GA, WK = 0.00104, 0.00135, 0.09
 
 
@@ -76,9 +79,10 @@ def psum(a):
 
 def build():
     P = []
+    cur = [""]
 
-    def add(qs, what, out, ins, args, cost, win=None):
-        P.append(dict(q=qs, what=what, out=out, ins=ins, args=args, cost=cost, w=spans(out) if out else [], r=[s for i in ins for s in spans(i)]))
+    def add(qs, what, out, ins, args, cost):
+        P.append(dict(b=cur[0], q=qs, what=what, out=out, ins=ins, args=args, cost=cost, w=(spans(out) if out else []) + (list(args) if what == "count" else []), r=[s for i in ins for s in spans(i)]))
 
     def ccost(out, ins, fast):
         n = width(out)
@@ -119,8 +123,8 @@ def build():
     def dma(q, out, a, sem):
         add(q, "dma", out, [a], (sem,), 0.06)
 
-    def iota(out, pat, cm):
-        add("G", "iota", out, [], (pat, cm), 0.13 + 2 * width(out) * CY)
+    def iota(out, pat, cm, base=0):
+        add("G", "iota", out, [], (pat, cm, base), 0.13 + 2 * width(out) * CY)
 
     def col(i):
         return X("COL", i, i + 1)
@@ -140,7 +144,6 @@ def build():
     iota(X("NG", 0, 256), [[1, 16], [0, 16]], 0)
     iota(X("NR", 0, 256), [[0, 16], [1, 16]], 0)
     iota(X("XW", X0 + XA, X0 + YMO), [[0, YMO - XA]], 0)
-    iota(X("EQ", 0, 2560), [[0, 2560]], 0)
     ts(X("TI", 0, 1), X("PI", 0, 1), 15, OP.bitwise_and)
     ts(X("TI", 1, 2), X("PI", 0, 1), 4, OP.arith_shift_right)
     tc(X("COL", 0, 2), X("TI", 0, 2))
@@ -163,6 +166,7 @@ def build():
     ts(col(17), col(5), 10, OP.mult)
     tt(col(10), col(16), col(17), OP.add)
     ts(col(18), pr, 1, OP.is_ge, -8192, OP.mult)
+    ts(col(19), pr, 1, OP.is_lt)
     tc(X("FDH", 0, 128), X("FAI", 0, 128))
     tc(X("FDH", 128, 256), X("DPI", 0, 128))
     for k in range(2):
@@ -170,7 +174,7 @@ def build():
             b = "b%d" % (4 * k + r // 4)
             mm(X(b, 128 * (r % 4), 128 * (r % 4) + 128), X("BSEL", 128 * r, 128 * r + 128), X("FDH", 128 * k, 128 * k + 128), True, True)
     for i in range(4):
-        act(X("F", 512 * i, 512 * i + 512), X("b%d" % i, 0, 512))
+        (act if FQ[i] == "A" else tc)(X("F", 512 * i, 512 * i + 512), X("b%d" % i, 0, 512))
     add("V", "ms", X("F", XA, XD), [], (2047.0,), 0.066)
     add("V", "ms", X("KD", XA, XD), [], (2047,), 0.066)
     ts(X("E1", 0, 128), G128, col(3), OP.mult)
@@ -185,7 +189,10 @@ def build():
         add("A", "sq", X("CM", 512 * i, 512 * i + 512), [X("b%d" % (4 + i), 0, 512), col(10)], (), 512 * CY)
         mm(X("b%d" % i, 0, 512), X("IDB", 0, 128), X("VAL", 512 * i, 512 * i + 512), True, False)
         mm(X("b%d" % i, 0, 512), X("IDM", 0, 128), X("CM", 512 * i, 512 * i + 512), False, True)
-        relu(X("M", 512 * i, 512 * i + 512), X("b%d" % i, 0, 512))
+        if MQ[i] == "A":
+            relu(X("M", 512 * i, 512 * i + 512), X("b%d" % i, 0, 512))
+        else:
+            ts(X("M", 512 * i, 512 * i + 512), X("b%d" % i, 0, 512), 0, OP.max)
     ts(X("TI", 0, 1), X("TI", 1, 2), 1, OP.bitwise_and)
     tc(col(14), X("TI", 0, 1))
     ts(col(13), col(14), -1, OP.mult, 1, OP.add)
@@ -199,32 +206,29 @@ def build():
     tc(X("LS", 0, 32), X("PU", 0, 32))
     ts(X("DM", 0, 256), X("NR", 0, 256), pr, OP.is_equal)
     ts(X("RMH", 0, 256), X("NR", 0, 256), 0, OP.not_equal)
-    ts(X("DLT", 0, 128), R128, pr, OP.subtract)
-    ts(X("E3", 0, 128), R128, 5, OP.is_le)
-    tt(X("BLK5", 0, 128), X("E3", 0, 128), X("BLK", 0, 128), OP.mult)
-    b5, dl, e1, e2, e3 = X("BLK5", 0, 128), X("DLT", 0, 128), X("E1", 0, 128), X("E2", 0, 128), X("E3", 0, 128)
     m128 = lambda n: X(n, 0, 128)
-    ts(e1, dl, 1, OP.is_equal, col(7), OP.mult)
-    ts(e2, dl, -4, OP.is_equal, col(4), OP.mult)
-    tt(e3, e1, e2, OP.add)
-    tt(m128("TA"), e3, b5, OP.mult)
+    dl, e3, s1, s2 = m128("DLT"), m128("E3"), m128("S1"), m128("S2")
+    ts(e3, R128, 5, OP.is_gt, 1000, OP.mult)
+    ts(m128("S3"), m128("BLK"), -1000, OP.mult, 1000, OP.add)
+    tt(m128("E4"), R128, e3, OP.add)
+    ts(X("E4", 128, 256), m128("E4"), pr, OP.subtract)
+    tt(dl, X("E4", 128, 256), m128("S3"), OP.add)
+    ts(s1, dl, 1, OP.is_equal, col(7), OP.mult)
+    ts(s2, dl, -4, OP.is_equal, col(4), OP.mult)
+    tt(m128("TA"), s1, s2, OP.add)
     ts(m128("TB"), m128("TA"), -1, OP.mult)
-    ts(e1, dl, -10, OP.is_le, col(8), OP.mult)
-    ts(e2, R128, 1, OP.is_ge)
-    tt(e3, e1, e2, OP.mult)
-    tt(m128("MS"), e3, b5, OP.mult)
-    ts(e1, dl, 0, OP.is_equal, col(7), OP.mult)
-    ts(e2, dl, -5, OP.is_equal, col(4), OP.mult)
-    tt(e3, e1, e2, OP.add)
-    tt(e1, e3, b5, OP.mult)
-    tt(m128("DMX"), e1, m128("TA"), OP.subtract)
-    ts(e1, dl, 1, OP.is_equal, col(6), OP.mult)
-    tt(m128("RT"), e1, b5, OP.mult)
+    ts(m128("MS"), dl, -10, OP.is_le, col(8), OP.mult)
+    ts(m128("S4"), dl, 0, OP.is_equal, col(7), OP.mult)
+    ts(m128("S5"), dl, -5, OP.is_equal, col(4), OP.mult)
+    tt(m128("S6"), m128("S4"), m128("S5"), OP.add)
+    tt(m128("DMX"), m128("S6"), m128("TA"), OP.subtract)
+    ts(m128("RT"), dl, 1, OP.is_equal, col(6), OP.mult)
     ts(m128("RTN"), m128("RT"), -1, OP.mult)
-    ts(e1, dl, 0, OP.is_equal, col(6), OP.mult)
-    tt(e2, e1, b5, OP.mult)
-    tt(m128("RD"), e2, m128("RT"), OP.subtract)
-    add("V", "ms", X("ZB", 0, 512), [], (0.0,), 0.27)
+    ts(X("S6", 128, 256), dl, 0, OP.is_equal, col(6), OP.mult)
+    tt(m128("RD"), X("S6", 128, 256), m128("RT"), OP.subtract)
+    iota(X("ZB", 0, 512), [[0, 512]], 0)
+    iota(X("RMB", 0, 1024), [[0, 64], [512, 16]], 0)
+    iota(X("KC", 0, 256), [[0, 16], [-1, 16]], 0, 15)
     ts(X("WBH", 0, 144), X("NF", 0, 144), 0, OP.mult)
     ts(X("WBH", 15, 143, 16), X("NF", 0, 8), pg, OP.is_equal)
     ts(X("WB16", 0, 144), X("WBH", 0, 144), 0.0625, OP.mult)
@@ -235,11 +239,7 @@ def build():
     ts(m128("IDN"), m128("IDB"), -1, OP.mult)
     ts(m128("ID2"), m128("IDB"), 2, OP.mult)
     tc(m128("IDH"), m128("IDB"))
-    tc(X("RMB", 0, 256), X("RMH", 0, 256))
-    tc(X("RMB", 256, 512), X("RMB", 0, 256))
-    tc(X("RMB", 512, 1024), X("RMB", 0, 512))
     ts(X("SEL", 0, 8), X("NF", 0, 8), pg, OP.is_equal, 16, OP.mult)
-    ts(X("KC", 0, 256), X("NR", 0, 256), -1, OP.mult, 15, OP.add)
     ts(col(11), pc, 0, OP.is_equal)
     ts(m128("E0"), N128, 0, OP.mult, col(11), OP.add)
     ts(X("L15", 0, 16), X("NF", 0, 16), 16, OP.mult, 15, OP.add)
@@ -251,10 +251,11 @@ def build():
     ts(X("QI", 16, 32), X("QI", 0, 16), 16, OP.arith_shift_right)
     ts(X("QF", 0, 16), X("QI", 16, 32), -7, OP.mult)
     tt(X("QF", 16, 32), X("QF", 0, 16), ln, OP.add)
-    for nm, base in (("BS1", -896), ("BS2", R2O)):
+    for i, (nm, base) in enumerate((("BS1", -896), ("BS2", R2O))):
         ts(X(nm, 0, 16), ln, YMO, OP.add)
         ts(X(nm, 16, 32), ln, ZMO, OP.add)
-        ts(X(nm, 32, 48), X("QF", 16, 32), 128, OP.mult, base, OP.add)
+        ts(X("RBK", 16 * i, 16 * i + 16), X("QF", 16, 32), 128, OP.mult, base, OP.add)
+    add("V", "ms", X("CNT", 0, 1), [], (0.0,), 0.066)
     ts(X("TBIG", 0, 256), X("NR", 0, 256), pr, OP.is_ge, 4096, OP.mult)
     ts(X("DUX", 0, 16), ln, XD, OP.add)
     ts(X("DUF", 0, 16), ln, XD, OP.add)
@@ -275,10 +276,10 @@ def build():
                     scan(X(*sc), X("RMH", 0, 256), g, OP.mult, OP.add)
                     tc(X("LS", 32 * k + 32 + 16 * s, 32 * k + 48 + 16 * s), X(sc[0], sc[1] + 15, sc[2], 16))
                 gm = X("GM", 512 * k + o, 512 * k + o + 256)
-                gat(gm, IND(mwin, ls))
+                gat(gm, IND(mwin, ls), "A" if last else GQ[2 * k + s])
                 if k == 4:
                     g5 = X("G5", o, o + 256)
-                    add("V", "tc", g5, [IND(X("F", 0, 2048), ls)], (), 0.05 + 256 * GA)
+                    gat(g5, IND(X("F", 0, 2048), ls), G5Q[2 * rnd + s])
                 mm(X("b0", 0, 256), m128("TB" if s else "TA"), gm, k == 0 and s == 0, k == 4 and s == 1 and False)
                 if k == 0:
                     mm(X("b0", 0, 256), m128("MS"), gm, False, False)
@@ -286,13 +287,16 @@ def build():
                 if k == 4:
                     mm(X("b0", 0, 256), m128("RTN" if s else "RT"), g5, False, s == 1)
                     mm(X("b1", o, o + 256), m128("RD"), g5, False, s == 1)
-        ts(X("VA", 0, 256), X("b0", 0, 256), col(18), OP.is_equal)
+        ts(X("VA", 0, 256), X("b0", 0, 256), col(18), OP.is_equal, col(19), OP.max)
         for s in range(2):
             tt(X("PR", 256 * s, 256 * s + 256), X("b1", 256 * s, 256 * s + 256), X("VA", 0, 256), OP.mult)
         for r in range(16):
             mm(X("b2", 0, 32), X("WBH", 15 - r, 143 - r), X("PR", r, 512, 16), r == 0, r == 15)
         tc(X("LA", 0, 32), X("b2", 0, 32))
         tc(X("AW", 0, 32), X("b2", 0, 32))
+        for r in range(16):
+            mm(X("b2", 32, 48), X("WBH", 15 - r, 143 - r), X("VA", r, 256, 16), r == 0, r == 15)
+        ts(X("W", 64, 80), X("b2", 32, 48), 2, OP.is_ge)
         mm(X("b3", 0, 512), m128("BLK"), X("PR", 0, 512), True, True)
         act(X("VALF", 256, 512), X("b3", 0, 256))
         act(X("VALF", 0, 256), X("b3", 256, 512))
@@ -311,6 +315,7 @@ def build():
             tc(X("KF", 256 * s, 256 * s + 256), X("KL", 256 * s, 256 * s + 256))
         for s in range(2):
             kb = "b%d" % (5 + s)
+            cur[0] = "mb" if s else "ma"
             mm(X(kb, 0, 256), m128("E0"), X("KC", 0, 256), True, False)
             for h in range(2):
                 base = 4096 * s + 2048 * h
@@ -331,7 +336,8 @@ def build():
         for s in range(2):
             o = 256 * s
             kb = "b%d" % (5 + s)
-            tc(X("KS", o, o + 256), X(kb, 0, 256))
+            cur[0] = "lb" if s else "la"
+            (act if KSA[s] == "A" else tc)(X("KS", o, o + 256), X(kb, 0, 256))
             scan(X("PS", o, o + 256), X("RMH", 0, 256), X("KS", o, o + 256), OP.mult, OP.max)
             tt(X("OHT", o, o + 256), IND(X("PS", o, o + 256), X("L15", 0, 16)), X("KS", o, o + 256), OP.is_equal)
             for h in range(2):
@@ -342,20 +348,22 @@ def build():
             tc(X("LL", 16 * s, 16 * s + 16), X("b3", 16 * s, 16 * s + 16))
             tc(X("LW", 16 * s, 16 * s + 16), X("b3", 16 * s, 16 * s + 16))
             tc(X("ZK", o, o + 256), IND(kwin, X("LL", 16 * s, 16 * s + 16)))
+            cur[0] = "zb" if s else "za"
             for q in range(4):
                 gat(X("Z", 4096 * s + 1024 * q, 4096 * s + 1024 * q + 1024), IND(xwin, X("ZK", o + 64 * q, o + 64 * q + 64)), "AV" if (s, q) in VG else "A")
             if not last:
                 act(X("OHS", o, o + 256), X("b7", o, o + 256))
         for n1, n2 in (("Y", "SY"), ("Z", "SZ")):
+            cur[0] = n2
             for s in range(2):
                 for q in range(4):
                     lo = 4096 * s + 1024 * q
-                    scan(X(n2, lo, lo + 1024), X("RMB", 0, 1024), X(n1, lo, lo + 1024), OP.mult, OP.max)
-        for s in range(2):
-            tc(X("FG", 256 * s, 256 * s + 256), IND(fwin, la(s)))
+                    scan(X(n2, lo, lo + 1024), X("RMB", 0, 1024), X(n1, lo, lo + 1024), OP.min, OP.max)
+        cur[0] = "co"
+        tc(X("FG", 0, 256), IND(fwin, la(0)))
         for r in range(16):
-            mm(X("b2", 0, 32), X("WB16", 15 - r, 143 - r), X("FG", r, 512, 16), r == 0, r == 15)
-        tc(X("FW", 0, 32), X("b2", 0, 32))
+            mm(X("b2", 0, 16), X("WB16", 15 - r, 143 - r), X("FG", r, 256, 16), r == 0, r == 15)
+        tc(X("FW", 0, 16), X("b2", 0, 16))
         tc(X("FWH", 0, 16), X("FW", 0, 16))
         mm(X("b2", 0, 256), m128("IDB"), X("TBIG", 0, 256), True, False)
         for r in range(16):
@@ -363,39 +371,38 @@ def build():
         tt(X("EQD", 0, 256), X("FG", 0, 256), X("b2", 0, 256), OP.is_equal)
         scan(X("SQD", 0, 256), X("RMH", 0, 256), X("EQD", 0, 256), OP.mult, OP.max)
         for c in range(1, 16):
-            k = c // 4
-            o = 128 * k * (k + 1) + (c - 4 * k) * 64 * (k + 1)
-            ts(X("EQ", o, o + 16 * c), X("FG", 0, 16 * c), X("FW", c, c + 1), OP.is_equal, c + 1, OP.mult)
-        scan(X("EQS", 0, 2560), X("EQ", 0, 2560), X("EQ", 0, 2560), OP.max, OP.max)
+            o = 8 * c * (c - 1)
+            ts(X("EQ", o, o + 16 * c), X("FG", 0, 16 * c), X("FW", c, c + 1), OP.is_equal)
+            add("A", "count", X("EQS", o, o + 16 * c), [X("EQ", o, o + 16 * c)], (X("CNT", c, c + 1),), max(64, 16 * c) * CY + 0.02)
 
         def w(i, n=1):
             return X("W", 16 * i, 16 * (i + n))
-        for k in range(4):
-            b = 128 * k * (k + 1)
-            n = 64 * (k + 1)
-            tt(X("W", 4 * k, 4 * k + 4), X("EQS", b + n - 1, b + 4 * n, n), X("NF", 1 + 4 * k, 5 + 4 * k), OP.not_equal)
-        ts(w(1), X("SQD", 15, 256, 16), 0, OP.is_equal)
-        tt(w(2), w(0), w(1), OP.mult)
+        tt(w(1), X("CNT", 0, 16), X("SQD", 15, 256, 16), OP.add)
+        ts(w(2), w(1), 0, OP.is_equal)
         tt(w(3), X("AW", 0, 16), X("AW", 16, 32), OP.not_equal)
-        tt(w(4), X("FW", 0, 16), X("FW", 16, 32), OP.is_equal)
         tt(w(5), w(3), w(4), OP.mult)
         tt(w(6), w(2), w(5), OP.mult)
         tt(w(7), w(2), w(6), OP.subtract)
         ts(w(12, 2), X("LW", 0, 32), 2047, OP.not_equal)
         tt(w(14), w(12), w(13), OP.mult)
         tt(w(15), w(14), w(6), OP.mult)
-        tc(w(8), X("AW", 0, 16))
-        tc(w(9), X("LW", 0, 16))
         tt(w(10), X("AW", 16, 32), X("AW", 0, 16), OP.subtract)
         tt(w(11), X("LW", 16, 32), X("LW", 0, 16), OP.subtract)
+        ts(w(26), w(5), -90, OP.mult, 99, OP.add)
+        ts(w(27), w(5), -90, OP.mult, 99, OP.add)
         tt(w(16, 2), X("LW", 0, 32), X("DUF", 0, 32), OP.subtract)
+        for i in range(2):
+            tt(w(16 + i), w(16 + i), w(15), OP.mult)
         if not last:
             tt(w(18, 2), X("AW", 0, 32), X("DUF", 0, 32), OP.subtract)
+            for i in range(2):
+                tt(w(18 + i), w(18 + i), w(15), OP.mult)
+        cur[0] = ""
         for i, src in enumerate(("SY", "SZ")):
             for r in range(16):
                 mm(X("b5", 0, 32), X("WBW", 15 - r, 143 - r), X(src, 15 + 16 * r, 8192, 256), i == 0 and r == 0, i == 1 and r == 15)
-        tc(X("XW", X0 + YMO, X0 + YMO + 256), X("SY", 15, 4096, 16))
-        tc(X("XW", X0 + ZMO, X0 + ZMO + 256), X("SZ", 15, 4096, 16))
+        act(X("XW", X0 + YMO, X0 + YMO + 256), X("SY", 15, 4096, 16))
+        act(X("XW", X0 + ZMO, X0 + ZMO + 256), X("SZ", 15, 4096, 16))
         for i, src in enumerate(("SY", "SZ")):
             for s in range(2):
                 mm(X("b6", 0, 256), m128("IDN" if s else "IDB"), X(src, 4096 * s + 15, 4096 * s + 4096, 16), i + s == 0, i + s == 2)
@@ -406,38 +413,38 @@ def build():
         tc(X("SI", 0, 32), X("b5", 0, 32))
         bs = "BS2" if last else "BS1"
         ts(X("SI", 32, 48), X("SI", 0, 16), 127, OP.bitwise_and)
-        tt(w(24), X("SI", 32, 48), X(bs, 32, 48), OP.add)
-        tc(w(22, 2), X(bs, 0, 32))
-        ts(w(20, 2), X("b2", 0, 32), 9, OP.is_ge)
+        tt(X(bs, 32, 48), X("SI", 32, 48), X("RBK", 16 * rnd, 16 * rnd + 16), OP.add)
+        for i in range(3):
+            tt(w(41 + i), X("LW" if i == 2 else "AW", 0, 16), X(bs, 16 * i, 16 * i + 16), OP.subtract)
+            tt(w(44 + i), X("LW" if i == 2 else "AW", 16, 32), X(bs, 16 * i, 16 * i + 16), OP.subtract)
+        tt(w(20, 2), X("b2", 0, 32), w(26, 2), OP.is_ge)
+        for i in range(6):
+            tt(w(48 + i), w(20 + i // 3), w(41 + i), OP.mult)
+        tt(w(54, 3), w(48, 3), w(51, 3), OP.add)
+        tt(w(57, 3), w(54, 3), X(bs, 0, 48), OP.add)
+        ts(X("LT", 0, 48), w(57, 3), 0 if last else X0, OP.add)
         tt(w(25), w(20), w(21), OP.add)
-        tt(w(26), w(21), w(5), OP.mult)
-        tt(w(27), w(21), w(5), OP.mult)
-        tt(w(30), w(25), w(15), OP.mult)
-        tt(w(28, 2), w(26, 2), w(10, 2), OP.mult)
-        tt(w(31), w(25), w(15), OP.mult)
-        tt(w(32, 2), w(28, 2), w(8, 2), OP.add)
-        tt(w(34, 2), w(30, 2), w(16, 2), OP.mult)
+        tt(w(34), w(25), w(16), OP.mult)
+        tt(w(35), w(25), w(17), OP.mult)
         tt(w(36, 2), w(34, 2), X("DUF", 0, 32), OP.add)
         tc(X("LF", 0, 32), w(36, 2))
         add("V", "tc", IND(X("F", 0, 2576), X("LF", 0, 32)), [X("VALF", 0, 512)], (), 0.05 + 512 * 0.0031)
-        for i in range(3):
-            tt(w(38 + i), w(25), w(5), OP.mult)
-        for i in range(3):
-            tt(w(41 + i), w(33 if i == 2 else 32), w(22 + i), OP.subtract)
-        tt(X("W", 704, 752), X("W", 608, 656), X("W", 656, 704), OP.mult)
-        tt(X("W", 656, 704), X("W", 704, 752), X("W", 352, 400), OP.add)
-        ts(X("LT", 0, 48), X("W", 656, 704), 0 if last else X0, OP.add)
+        tt(w(28), w(21), w(10), OP.mult)
+        tt(w(32), w(28), X("AW", 0, 16), OP.add)
+        if not last:
+            tt(w(29), w(21), w(11), OP.mult)
+            tt(w(33), w(29), X("LW", 0, 16), OP.add)
         twin = X("XW", X0, X0 + XEND) if last else X("XW", 0, X0 + R2O)
         for i in range(3):
             gat(X("TG", 256 * i, 256 * i + 256), IND(twin, X("LT", 16 * i, 16 * i + 16)), "AV")
         for i in range(3):
             mm(X("b3", 0, 256), m128("ID2" if i == 2 else "IDB"), X("TG", 256 * i, 256 * i + 256), i == 0, i == 2)
-        tt(w(28), w(6), w(25), OP.mult)
-        tt(w(29), w(28), w(7), OP.add)
-        tt(w(28), w(32), X("DUX", 0, 16), OP.subtract)
-        tt(w(34), w(28), w(29), OP.mult)
-        tt(w(35), w(34), X("DUX", 0, 16), OP.add)
-        tc(X("LX", 0, 16), w(35))
+        tt(w(38), w(2), w(25), OP.mult)
+        tt(w(39), w(38), w(7), OP.add)
+        tt(w(60), w(32), X("DUX", 0, 16), OP.subtract)
+        tt(w(61), w(60), w(39), OP.mult)
+        tt(w(62), w(61), X("DUX", 0, 16), OP.add)
+        tc(X("LX", 0, 16), w(62))
         ts(X("VI", 0, 256), X("b3", 0, 256), 0.25, OP.mult, -0.375, OP.add)
         add("W", "waitsent", X("XW", X0, X0 + 128), [], (rnd + 1,), 0)
         add("V", "tc", IND(X("XW", X0, X0 + YMO), X("LX", 0, 16)), [X("VI", 0, 256)], (), 0.05 + 256 * 0.0031)
@@ -448,18 +455,18 @@ def build():
             break
         add("G", "send", None, [X("XW", X0, X0 + 128)], (2,), 1.0)
         add("N", "arrive", X("XW", X0 + R2O, X0 + XEND), [], (2,), 0)
-        ts(w(28), w(33), 2047, OP.is_equal)
-        tt(w(29), w(32), w(33), OP.subtract)
-        tt(w(34), w(28), w(29), OP.mult)
-        tt(w(35), w(34), w(33), OP.add)
-        tc(X("LS", 0, 16), w(35))
+        ts(w(63), w(33), 2047, OP.is_equal)
+        tt(w(64), w(32), w(33), OP.subtract)
+        tt(w(65), w(63), w(64), OP.mult)
+        tt(w(66), w(65), w(33), OP.add)
+        tc(X("LS", 0, 16), w(66))
         for s in range(2):
             tt(X("KDD", 64 * s, 64 * s + 64), X("KF", 256 * s, 256 * s + 64), X("DM", 0, 64), OP.mult)
         scan(X("KDS", 0, 128), X("RMH", 0, 128), X("KDD", 0, 128), OP.mult, OP.add)
         tc(X("KN", 0, 8), X("KDS", 15, 128, 16))
-        tt(X("W", 704, 708), X("KN", 4, 8), X("KN", 0, 4), OP.subtract)
-        tt(X("W", 708, 712), X("W", 704, 708), X("W", 416, 420), OP.mult)
-        tt(X("LSI", 0, 4), X("W", 708, 712), X("KN", 0, 4), OP.add)
+        tt(X("W", 1072, 1076), X("KN", 4, 8), X("KN", 0, 4), OP.subtract)
+        tt(X("W", 1076, 1080), X("W", 1072, 1076), X("W", 336, 340), OP.mult)
+        tt(X("LSI", 0, 4), X("W", 1076, 1080), X("KN", 0, 4), OP.add)
         tt(X("SI", 48, 64), X("SI", 0, 16), X("SI", 16, 32), OP.add)
         tt(X("LSI", 16, 32), X("SI", 48, 64), X("L977", 0, 16), OP.add)
         ts(X("LSI", 4, 16), X("LSI", 20, 32), 2047, OP.bitwise_and)
@@ -472,9 +479,10 @@ def build():
         mm(X("b4", 0, 512), m128("IDH"), X("TK", 0, 512), True, False)
         mm(X("b4", 0, 512), m128("IDH"), X("KF", 0, 512), False, True)
         act(X("NK", 0, 512), X("b4", 0, 512))
-        tt(w(34, 2), w(30, 2), w(18, 2), OP.mult)
-        tt(w(36, 2), w(34, 2), X("DUF", 0, 32), OP.add)
-        tc(X("LF", 32, 64), w(36, 2))
+        for i in range(2):
+            tt(w(68 + i), w(25), w(18 + i), OP.mult)
+        tt(w(70, 2), w(68, 2), X("DUF", 0, 32), OP.add)
+        tc(X("LF", 32, 64), w(70, 2))
         add("V", "tc", IND(X("KD", 0, 2576), X("LF", 32, 64)), [X("NK", 0, 512)], (), 0.05 + 512 * 0.0031)
     return P
 
@@ -521,7 +529,7 @@ def order(P, preds):
         for i, t in ready.items():
             qs = P[i]["q"]
             q = min(qs, key=lambda z: max(free[z], t)) if len(qs) > 1 else qs
-            cand.append((max(free[q], t), -prio[i], i, q))
+            cand.append((max(free[q], t), -prio[i] - BOOST.get(P[i]["b"], 0.0), i, q))
         first = min(cand)
         st, _, i, q = min((c for c in cand if c[3] == first[3] and c[0] <= first[0] + SLACK), key=lambda c: (c[1], c[0]))
         queue[i] = q
@@ -633,6 +641,8 @@ def rank_program(g, core, T, topo):
             h = e.tensor_copy(out, ins[0])
         elif what == "gat":
             h = e.activation(out, ins[0], AF.Copy)
+        elif what == "count":
+            h = e.activation(out, ins[0], AF.Copy, accum_out=ap(args[0]))
         elif what == "sq":
             h = e.activation(out, ins[0], AF.Square, bias=ins[1])
         elif what == "relu":
@@ -653,7 +663,7 @@ def rank_program(g, core, T, topo):
         elif what == "ms":
             h = e.memset(out, args[0])
         elif what == "iota":
-            h = e.iota(out, args[0], 0, args[1], allow_small_or_imprecise_dtypes=True)
+            h = e.iota(out, args[0], args[2], args[1], allow_small_or_imprecise_dtypes=True)
         h.then_inc(T.sem["q" + q], 1)
         count[q] += 1
         done[i] = [("q" + q, count[q])]

from concourse.bass import DstId, RemoteDMATransfer
from concourse.mybir import AluOpType as OP, ActivationFunctionType as AF

X0, XA, XD, YMO, ZMO, R2O = 896, 2048, 2064, 2320, 2576, 2832
XEND = R2O + 896
ND = 4

SCRATCH = {}
for _n, _w, _d in (
        ("XW", X0 + XEND, "bfloat16"), ("KD", 2576, "int32"), ("F", 2576, "float32"), ("M", 2048, "bfloat16"), ("VAL", 2048, "bfloat16"), ("CM", 2048, "bfloat16"),
        ("FAI", 128, "int32"), ("DPI", 128, "int32"), ("PAI", 16, "int32"), ("PBI", 16, "int32"), ("WTI", 1, "int32"), ("FDH", 256, "float16"),
        ("PI", 1, "int32"), ("TI", 2, "int32"), ("COL", 32, "float32"), ("NF", 256, "float32"), ("NR", 256, "float32"), ("NG", 256, "float32"),
        ("BLK", 128, "float16"), ("NBLK", 128, "float16"), ("WBH", 144, "float16"), ("WB16", 144, "float16"), ("WBB", 144, "bfloat16"), ("WBW", 144, "bfloat16"),
        ("IDB", 128, "bfloat16"), ("IDN", 128, "bfloat16"), ("ID2", 128, "bfloat16"), ("IDH", 128, "float16"), ("IDM", 128, "bfloat16"), ("BSEL", 2048, "float16"), ("DELR", 16, "float32"), ("B8", 16, "float32"),
        ("DM", 256, "bfloat16"), ("RMH", 256, "float16"), ("RMB", 1024, "bfloat16"), ("SEL", 8, "bfloat16"), ("KC", 256, "bfloat16"), ("E0", 128, "bfloat16"), ("ZB", 512, "bfloat16"),
        ("L15", 16, "uint16"), ("DLT", 128, "bfloat16"), ("S1", 128, "bfloat16"), ("S2", 128, "bfloat16"), ("S3", 128, "bfloat16"), ("S4", 128, "bfloat16"), ("S5", 128, "bfloat16"), ("S6", 256, "bfloat16"), ("E4", 256, "float32"), ("E1", 128, "float32"), ("E2", 128, "float32"), ("E3", 128, "float32"), ("P0", 128, "float32"),
        ("TA", 128, "bfloat16"), ("TB", 128, "bfloat16"), ("DMX", 128, "bfloat16"), ("MS", 128, "bfloat16"), ("RT", 128, "bfloat16"), ("RTN", 128, "bfloat16"), ("RD", 128, "bfloat16"),
        ("LN", 16, "float32"), ("L977", 16, "float32"), ("QI", 32, "int32"), ("QF", 32, "float32"), ("TBIG", 256, "bfloat16"), ("DUX", 16, "float32"), ("DUF", 32, "float32"),
        ("RBK", 32, "float32"), ("CNT", 16, "float32"), ("BS1", 48, "float32"), ("BS2", 48, "float32"), ("EQ", 2560, "bfloat16"), ("EQS", 2560, "bfloat16"), ("PX", 64, "float32"), ("PT", 64, "float32"), ("PU", 32, "float32"),
        ("GM", 2560, "bfloat16"), ("G5", 512, "bfloat16"), ("G", 2048, "float16"), ("SC", 2048, "float16"), ("LS", 160, "uint16"), ("LSI", 32, "int32"),
        ("VA", 256, "float16"), ("PR", 512, "float16"), ("AW", 32, "float32"), ("LA", 32, "uint16"), ("VALF", 512, "float32"),
        ("KL", 512, "uint16"), ("KF", 512, "float16"), ("XS", 512, "bfloat16"), ("Y", 8192, "bfloat16"), ("SY", 8192, "bfloat16"), ("MM", 8192, "bfloat16"),
        ("KS", 512, "float32"), ("PS", 512, "float32"), ("OHT", 512, "bfloat16"), ("OHS", 512, "bfloat16"), ("PL", 512, "float16"), ("LL", 32, "uint16"), ("LW", 32, "float32"),
        ("ZK", 512, "uint16"), ("Z", 8192, "bfloat16"), ("SZ", 8192, "bfloat16"), ("FG", 512, "float16"), ("FW", 32, "float32"), ("FWH", 16, "float16"),
        ("EQD", 256, "bfloat16"), ("SQD", 256, "bfloat16"), ("GL", 512, "bfloat16"), ("W", 1152, "float32"), ("SI", 64, "int32"), ("KDD", 128, "float16"), ("KDS", 128, "float16"), ("KN", 8, "float32"),
        ("LT", 48, "uint16"), ("LX", 16, "uint16"), ("LF", 64, "uint16"), ("TG", 768, "bfloat16"), ("VI", 256, "int32"), ("TK", 512, "float16"), ("NK", 512, "float32")):
    SCRATCH[_n] = ("sbuf", [128, _w], _d)
for _b in range(8):
    SCRATCH["b%d" % _b] = ("psum", [128, 512], "float32")
SEMAPHORES = ["qV", "qA", "qT", "qG", "sent1", "sent2", "arr1", "arr2"] + ["d%d" % _i for _i in range(12)]

VY = ((1, 0),)
RELU = ((1, 0),)
VG = ((0, 0), (1, 1), (1, 3))
SLACK = 0.0
KSA, FQ, MQ, GQ = "VA", "VAAV", "AAVA", "AAAAAAAAVA"
BOOST = {"ma": 6.0, "la": 20.0, "lb": -2.0, "SZ": 32.0, "zb": -4.0, "za": -4.0}
G5Q = "AAAA"
CY, GA, WK = 0.00104, 0.00135, 0.09


def X(name, lo, hi, st=1, p0=0, p1=128):
    return ("x", name, lo, hi, st, p0, p1)


def IND(win, off):
    return ("i", win, off)


def width(a):
    if a[0] == "i":
        return 16 * (a[2][3] - a[2][2])
    return (a[3] - a[2] + a[4] - 1) // a[4]


def spans(a):
    return [a[1], a[2]] if a[0] == "i" else [a]


def gcd(a, b):
    while b:
        a, b = b, a % b
    return a


def clash(a, b):
    if a[2] >= b[3] or b[2] >= a[3] or a[5] >= b[6] or b[5] >= a[6]:
        return False
    return (a[2] - b[2]) % gcd(a[4], b[4]) == 0


def two(a):
    return a[0] == "x" and a[1][0] != "b" and SCRATCH[a[1]][2] in ("bfloat16", "float16", "uint16")


def psum(a):
    return a[0] == "x" and a[1][0] == "b"


def build():
    P = []
    cur = [""]

    def add(qs, what, out, ins, args, cost):
        P.append(dict(b=cur[0], q=qs, what=what, out=out, ins=ins, args=args, cost=cost, w=(spans(out) if out else []) + (list(args) if what == "count" else []), r=[s for i in ins for s in spans(i)]))

    def ccost(out, ins, fast):
        n = width(out)
        if out[0] == "i":
            return 0.05 + n * 0.0031
        if ins[0][0] == "i":
            return 0.05 + n * GA
        return max(64, n * (0.5 if fast and two(out) and all(two(i) for i in ins) else 1)) * CY

    def tc(out, a, q="V"):
        add(q, "tc", out, [a], (), ccost(out, [a], True))

    def tt(out, a, b, op):
        n = width(b)
        c = 0.05 + n * GA if a[0] == "i" else max(64, n * (1 if psum(a) or psum(b) else 2)) * CY
        add("V", "tt", out, [a, b], (op,), c)

    def ts(out, a, s1, o1, s2=None, o2=None):
        ins = [a] + [s for s in (s1, s2) if isinstance(s, tuple)]
        add("V", "ts", out, ins, (s1, o1, s2, o2), ccost(out, [a], True))

    def scan(out, d0, d1, o0, o1):
        add("V", "scan", out, [d0, d1], (o0, o1), ccost(out, [d0, d1], True))

    def act(out, a, bias=None):
        c = 0.065 + width(out) * GA if a[0] == "i" else max(64, width(out)) * CY
        add("A", "act", out, [a] + ([bias] if bias else []), (bias,), c)

    def relu(out, a):
        add("A", "relu", out, [a], (), width(out) * CY)

    def gat(out, a, q="A"):
        add(q, "gat", out, [a], (), 0.06 + width(out) * GA)

    def mm(out, l, r, start, stop):
        add("T", "mm", out, [l, r], (start, stop), max(64, width(r)) * CY)

    def dma(q, out, a, sem):
        add(q, "dma", out, [a], (sem,), 0.06)

    def iota(out, pat, cm, base=0):
        add("G", "iota", out, [], (pat, cm, base), 0.13 + 2 * width(out) * CY)

    def col(i):
        return X("COL", i, i + 1)

    dma("S", X("FAI", 0, 128), ("d", "fa"), "d0")
    dma("A", X("DPI", 0, 128), ("d", "dp"), "d1")
    dma("S", X("PAI", 0, 16), ("d", "pa"), "d2")
    dma("A", X("PBI", 0, 16), ("d", "pb"), "d3")
    dma("S", X("KD", 0, 2048), ("d", "kd"), "d5")
    dma("S", X("XW", X0, X0 + 2048), ("d", "xs"), "d6")
    dma("S", X("WTI", 0, 1), ("d", "wt"), "d4")
    add("G", "send", None, [X("XW", X0, X0 + 128)], (1,), 1.0)
    add("N", "arrive", X("XW", 0, 896), [], (1,), 0)

    iota(X("PI", 0, 1), [[0, 1]], 1)
    iota(X("NF", 0, 256), [[1, 256]], 0)
    iota(X("NG", 0, 256), [[1, 16], [0, 16]], 0)
    iota(X("NR", 0, 256), [[0, 16], [1, 16]], 0)
    iota(X("XW", X0 + XA, X0 + YMO), [[0, YMO - XA]], 0)
    ts(X("TI", 0, 1), X("PI", 0, 1), 15, OP.bitwise_and)
    ts(X("TI", 1, 2), X("PI", 0, 1), 4, OP.arith_shift_right)
    tc(X("COL", 0, 2), X("TI", 0, 2))
    tc(col(2), X("PI", 0, 1))
    N128, R128, G128 = X("NF", 0, 128), X("NR", 0, 128), X("NG", 0, 128)
    pr, pg, pc = col(0), col(1), col(2)
    ts(X("BLK", 0, 128), G128, pg, OP.is_equal)
    ts(X("DELR", 0, 16), X("NF", 0, 16), pr, OP.is_equal)
    for r in range(16):
        ts(X("BSEL", 128 * r, 128 * r + 128), X("BLK", 0, 128), X("DELR", r, r + 1), OP.mult)
    ts(col(6), pr, 1, OP.is_lt)
    ts(col(15), pr, 6, OP.is_ge)
    ts(col(5), pr, 11, OP.is_ge)
    ts(col(3), pr, 1, OP.is_ge)
    tt(col(3), col(3), col(15), OP.subtract)
    tt(col(4), col(15), col(5), OP.subtract)
    ts(col(7), col(3), 16, OP.mult)
    ts(col(8), col(5), -4096, OP.mult)
    ts(col(16), col(4), 5, OP.mult, pr, OP.subtract)
    ts(col(17), col(5), 10, OP.mult)
    tt(col(10), col(16), col(17), OP.add)
    ts(col(18), pr, 1, OP.is_ge, -8192, OP.mult)
    ts(col(19), pr, 1, OP.is_lt)
    tc(X("FDH", 0, 128), X("FAI", 0, 128))
    tc(X("FDH", 128, 256), X("DPI", 0, 128))
    for k in range(2):
        for r in range(16):
            b = "b%d" % (4 * k + r // 4)
            mm(X(b, 128 * (r % 4), 128 * (r % 4) + 128), X("BSEL", 128 * r, 128 * r + 128), X("FDH", 128 * k, 128 * k + 128), True, True)
    for i in range(4):
        (act if FQ[i] == "A" else tc)(X("F", 512 * i, 512 * i + 512), X("b%d" % i, 0, 512))
    add("V", "ms", X("F", XA, XD), [], (2047.0,), 0.066)
    add("V", "ms", X("KD", XA, XD), [], (2047,), 0.066)
    ts(X("E1", 0, 128), G128, col(3), OP.mult)
    ts(X("E2", 0, 128), R128, col(4), OP.mult, col(5), OP.add)
    tt(X("P0", 0, 128), X("E1", 0, 128), X("E2", 0, 128), OP.add)
    ts(X("B8", 0, 16), X("NF", 0, 16), 8, OP.mult, col(3), OP.mult)
    for r in range(16):
        act(X("VAL", 128 * r, 128 * r + 128), X("P0", 0, 128), X("B8", r, r + 1))
    ts(X("IDB", 0, 128), N128, pc, OP.is_equal)
    ts(X("IDM", 0, 128), X("IDB", 0, 128), -256, OP.mult)
    for i in range(4):
        add("A", "sq", X("CM", 512 * i, 512 * i + 512), [X("b%d" % (4 + i), 0, 512), col(10)], (), 512 * CY)
        mm(X("b%d" % i, 0, 512), X("IDB", 0, 128), X("VAL", 512 * i, 512 * i + 512), True, False)
        mm(X("b%d" % i, 0, 512), X("IDM", 0, 128), X("CM", 512 * i, 512 * i + 512), False, True)
        if MQ[i] == "A":
            relu(X("M", 512 * i, 512 * i + 512), X("b%d" % i, 0, 512))
        else:
            ts(X("M", 512 * i, 512 * i + 512), X("b%d" % i, 0, 512), 0, OP.max)
    ts(X("TI", 0, 1), X("TI", 1, 2), 1, OP.bitwise_and)
    tc(col(14), X("TI", 0, 1))
    ts(col(13), col(14), -1, OP.mult, 1, OP.add)
    for s in range(2):
        src = X("PBI" if s else "PAI", 0, 16)
        ts(X("PX", 32 * s, 32 * s + 16), src, col(13), OP.mult)
        ts(X("PX", 32 * s + 16, 32 * s + 32), src, col(14), OP.mult)
    add("V", "tr", X("PT", 0, 64), [X("PX", 0, 64)], (), 0.07)
    for s in range(2):
        tt(X("PU", 16 * s, 16 * s + 16), X("PT", 32 * s, 32 * s + 16), X("PT", 32 * s + 16, 32 * s + 32), OP.add)
    tc(X("LS", 0, 32), X("PU", 0, 32))
    ts(X("DM", 0, 256), X("NR", 0, 256), pr, OP.is_equal)
    ts(X("RMH", 0, 256), X("NR", 0, 256), 0, OP.not_equal)
    m128 = lambda n: X(n, 0, 128)
    dl, e3, s1, s2 = m128("DLT"), m128("E3"), m128("S1"), m128("S2")
    ts(e3, R128, 5, OP.is_gt, 1000, OP.mult)
    ts(m128("S3"), m128("BLK"), -1000, OP.mult, 1000, OP.add)
    tt(m128("E4"), R128, e3, OP.add)
    ts(X("E4", 128, 256), m128("E4"), pr, OP.subtract)
    tt(dl, X("E4", 128, 256), m128("S3"), OP.add)
    ts(s1, dl, 1, OP.is_equal, col(7), OP.mult)
    ts(s2, dl, -4, OP.is_equal, col(4), OP.mult)
    tt(m128("TA"), s1, s2, OP.add)
    ts(m128("TB"), m128("TA"), -1, OP.mult)
    ts(m128("MS"), dl, -10, OP.is_le, col(8), OP.mult)
    ts(m128("S4"), dl, 0, OP.is_equal, col(7), OP.mult)
    ts(m128("S5"), dl, -5, OP.is_equal, col(4), OP.mult)
    tt(m128("S6"), m128("S4"), m128("S5"), OP.add)
    tt(m128("DMX"), m128("S6"), m128("TA"), OP.subtract)
    ts(m128("RT"), dl, 1, OP.is_equal, col(6), OP.mult)
    ts(m128("RTN"), m128("RT"), -1, OP.mult)
    ts(X("S6", 128, 256), dl, 0, OP.is_equal, col(6), OP.mult)
    tt(m128("RD"), X("S6", 128, 256), m128("RT"), OP.subtract)
    iota(X("ZB", 0, 512), [[0, 512]], 0)
    iota(X("RMB", 0, 1024), [[0, 64], [512, 16]], 0)
    iota(X("KC", 0, 256), [[0, 16], [-1, 16]], 0, 15)
    ts(X("WBH", 0, 144), X("NF", 0, 144), 0, OP.mult)
    ts(X("WBH", 15, 143, 16), X("NF", 0, 8), pg, OP.is_equal)
    ts(X("WB16", 0, 144), X("WBH", 0, 144), 0.0625, OP.mult)
    tc(X("WBB", 0, 144), X("WBH", 0, 144))
    tc(col(12), X("WTI", 0, 1))
    ts(X("WBW", 0, 144), X("WBB", 0, 144), col(12), OP.mult)
    ts(m128("NBLK"), m128("BLK"), -1, OP.mult)
    ts(m128("IDN"), m128("IDB"), -1, OP.mult)
    ts(m128("ID2"), m128("IDB"), 2, OP.mult)
    tc(m128("IDH"), m128("IDB"))
    ts(X("SEL", 0, 8), X("NF", 0, 8), pg, OP.is_equal, 16, OP.mult)
    ts(col(11), pc, 0, OP.is_equal)
    ts(m128("E0"), N128, 0, OP.mult, col(11), OP.add)
    ts(X("L15", 0, 16), X("NF", 0, 16), 16, OP.mult, 15, OP.add)
    n16 = X("NF", 0, 16)
    ts(X("LN", 0, 16), n16, 16, OP.mult, pr, OP.add)
    ln = X("LN", 0, 16)
    ts(X("L977", 0, 16), ln, 977, OP.mult)
    ts(X("QI", 0, 16), ln, 9363, OP.mult)
    ts(X("QI", 16, 32), X("QI", 0, 16), 16, OP.arith_shift_right)
    ts(X("QF", 0, 16), X("QI", 16, 32), -7, OP.mult)
    tt(X("QF", 16, 32), X("QF", 0, 16), ln, OP.add)
    for i, (nm, base) in enumerate((("BS1", -896), ("BS2", R2O))):
        ts(X(nm, 0, 16), ln, YMO, OP.add)
        ts(X(nm, 16, 32), ln, ZMO, OP.add)
        ts(X("RBK", 16 * i, 16 * i + 16), X("QF", 16, 32), 128, OP.mult, base, OP.add)
    add("V", "ms", X("CNT", 0, 1), [], (0.0,), 0.066)
    ts(X("TBIG", 0, 256), X("NR", 0, 256), pr, OP.is_ge, 4096, OP.mult)
    ts(X("DUX", 0, 16), ln, XD, OP.add)
    ts(X("DUF", 0, 16), ln, XD, OP.add)
    ts(X("DUF", 16, 32), ln, XD + 256, OP.add)

    xwin, kwin, fwin, mwin = X("XW", X0, X0 + XD), X("KD", 0, XD), X("F", 0, XD), X("M", 0, 2048)
    for rnd in range(2):
        last = rnd == 1
        mm(X("b1", 0, 512), m128("IDB"), X("ZB", 0, 512), True, False)
        for k in range(5):
            for s in range(2):
                ls = X("LS", 32 * k + 16 * s, 32 * k + 16 * s + 16)
                o = 256 * s
                if k < 4:
                    g = X("G", 512 * k + o, 512 * k + o + 256)
                    sc = ("SC", 512 * k + o, 512 * k + o + 256)
                    tt(g, IND(X("F", 0, 2048), ls), X("DM", 0, 256), OP.mult)
                    scan(X(*sc), X("RMH", 0, 256), g, OP.mult, OP.add)
                    tc(X("LS", 32 * k + 32 + 16 * s, 32 * k + 48 + 16 * s), X(sc[0], sc[1] + 15, sc[2], 16))
                gm = X("GM", 512 * k + o, 512 * k + o + 256)
                gat(gm, IND(mwin, ls), "A" if last else GQ[2 * k + s])
                if k == 4:
                    g5 = X("G5", o, o + 256)
                    gat(g5, IND(X("F", 0, 2048), ls), G5Q[2 * rnd + s])
                mm(X("b0", 0, 256), m128("TB" if s else "TA"), gm, k == 0 and s == 0, k == 4 and s == 1 and False)
                if k == 0:
                    mm(X("b0", 0, 256), m128("MS"), gm, False, False)
                mm(X("b1", o, o + 256), m128("DMX"), gm, False, False)
                if k == 4:
                    mm(X("b0", 0, 256), m128("RTN" if s else "RT"), g5, False, s == 1)
                    mm(X("b1", o, o + 256), m128("RD"), g5, False, s == 1)
        ts(X("VA", 0, 256), X("b0", 0, 256), col(18), OP.is_equal, col(19), OP.max)
        for s in range(2):
            tt(X("PR", 256 * s, 256 * s + 256), X("b1", 256 * s, 256 * s + 256), X("VA", 0, 256), OP.mult)
        for r in range(16):
            mm(X("b2", 0, 32), X("WBH", 15 - r, 143 - r), X("PR", r, 512, 16), r == 0, r == 15)
        tc(X("LA", 0, 32), X("b2", 0, 32))
        tc(X("AW", 0, 32), X("b2", 0, 32))
        for r in range(16):
            mm(X("b2", 32, 48), X("WBH", 15 - r, 143 - r), X("VA", r, 256, 16), r == 0, r == 15)
        ts(X("W", 64, 80), X("b2", 32, 48), 2, OP.is_ge)
        mm(X("b3", 0, 512), m128("BLK"), X("PR", 0, 512), True, True)
        act(X("VALF", 256, 512), X("b3", 0, 256))
        act(X("VALF", 0, 256), X("b3", 256, 512))

        def la(s):
            return X("LA", 16 * s, 16 * s + 16)
        for s in range(2):
            gat(X("XS", 256 * s, 256 * s + 256), IND(xwin, la(s)))
            mm(X("b4", 256 - 256 * s, 512 - 256 * s), m128("IDB"), X("XS", 256 * s, 256 * s + 256), True, True)
        for s in range(2):
            tc(X("KL", 256 * s, 256 * s + 256), IND(kwin, la(s)))
        for s in range(2):
            for q in range(4):
                gat(X("Y", 4096 * s + 1024 * q, 4096 * s + 1024 * q + 1024), IND(xwin, X("KL", 256 * s + 64 * q, 256 * s + 64 * q + 64)), "V" if (s, q) in VY else "A")
        for s in range(2):
            tc(X("KF", 256 * s, 256 * s + 256), X("KL", 256 * s, 256 * s + 256))
        for s in range(2):
            kb = "b%d" % (5 + s)
            cur[0] = "mb" if s else "ma"
            mm(X(kb, 0, 256), m128("E0"), X("KC", 0, 256), True, False)
            for h in range(2):
                base = 4096 * s + 2048 * h
                for i in range(4):
                    for j in range(4 * i, 4 * i + 4):
                        y, m = X("Y", base + j, base + 2048, 16), X("MM", base + 128 * j, base + 128 * j + 128)
                        if (s, h) in RELU:
                            b = "b%d" % (i % 2)
                            c = 128 * (j - 4 * i)
                            mm(X(b, c, c + 128), m128("IDB"), y, True, False)
                            mm(X(b, c, c + 128), m128("IDN"), X("XS", 256 - 256 * s + 128 * h, 384 - 256 * s + 128 * h), False, True)
                        else:
                            tt(m, y, X("b4", 256 * s + 128 * h, 256 * s + 128 * h + 128), OP.max)
                    if (s, h) in RELU:
                        relu(X("MM", base + 512 * i, base + 512 * i + 512), X("b%d" % (i % 2), 0, 512))
                    for j in range(4 * i, 4 * i + 4):
                        mm(X(kb, 128 * h + j, 128 * h + 128, 16), X("MM", base + 128 * j, base + 128 * j + 128), X("SEL", 0, 8), False, h == 1 and j == 15)
        for s in range(2):
            o = 256 * s
            kb = "b%d" % (5 + s)
            cur[0] = "lb" if s else "la"
            (act if KSA[s] == "A" else tc)(X("KS", o, o + 256), X(kb, 0, 256))
            scan(X("PS", o, o + 256), X("RMH", 0, 256), X("KS", o, o + 256), OP.mult, OP.max)
            tt(X("OHT", o, o + 256), IND(X("PS", o, o + 256), X("L15", 0, 16)), X("KS", o, o + 256), OP.is_equal)
            for h in range(2):
                mm(X("b7", o + 128 * h, o + 128 * h + 128), X("OHT", o + 128 * h, o + 128 * h + 128), m128("IDB"), True, True)
            tt(X("PL", o, o + 256), X("b7", o, o + 256), X("KF", o, o + 256), OP.mult)
            for r in range(16):
                mm(X("b3", 16 * s, 16 * s + 16), X("WBH", 15 - r, 143 - r), X("PL", o + r, o + 256, 16), r == 0, r == 15)
            tc(X("LL", 16 * s, 16 * s + 16), X("b3", 16 * s, 16 * s + 16))
            tc(X("LW", 16 * s, 16 * s + 16), X("b3", 16 * s, 16 * s + 16))
            tc(X("ZK", o, o + 256), IND(kwin, X("LL", 16 * s, 16 * s + 16)))
            cur[0] = "zb" if s else "za"
            for q in range(4):
                gat(X("Z", 4096 * s + 1024 * q, 4096 * s + 1024 * q + 1024), IND(xwin, X("ZK", o + 64 * q, o + 64 * q + 64)), "AV" if (s, q) in VG else "A")
            if not last:
                act(X("OHS", o, o + 256), X("b7", o, o + 256))
        for n1, n2 in (("Y", "SY"), ("Z", "SZ")):
            cur[0] = n2
            for s in range(2):
                for q in range(4):
                    lo = 4096 * s + 1024 * q
                    scan(X(n2, lo, lo + 1024), X("RMB", 0, 1024), X(n1, lo, lo + 1024), OP.min, OP.max)
        cur[0] = "co"
        tc(X("FG", 0, 256), IND(fwin, la(0)))
        for r in range(16):
            mm(X("b2", 0, 16), X("WB16", 15 - r, 143 - r), X("FG", r, 256, 16), r == 0, r == 15)
        tc(X("FW", 0, 16), X("b2", 0, 16))
        tc(X("FWH", 0, 16), X("FW", 0, 16))
        mm(X("b2", 0, 256), m128("IDB"), X("TBIG", 0, 256), True, False)
        for r in range(16):
            mm(X("b2", r, 256, 16), m128("IDH"), X("FWH", 0, 16), False, r == 15)
        tt(X("EQD", 0, 256), X("FG", 0, 256), X("b2", 0, 256), OP.is_equal)
        scan(X("SQD", 0, 256), X("RMH", 0, 256), X("EQD", 0, 256), OP.mult, OP.max)
        for c in range(1, 16):
            o = 8 * c * (c - 1)
            ts(X("EQ", o, o + 16 * c), X("FG", 0, 16 * c), X("FW", c, c + 1), OP.is_equal)
            add("A", "count", X("EQS", o, o + 16 * c), [X("EQ", o, o + 16 * c)], (X("CNT", c, c + 1),), max(64, 16 * c) * CY + 0.02)

        def w(i, n=1):
            return X("W", 16 * i, 16 * (i + n))
        tt(w(1), X("CNT", 0, 16), X("SQD", 15, 256, 16), OP.add)
        ts(w(2), w(1), 0, OP.is_equal)
        tt(w(3), X("AW", 0, 16), X("AW", 16, 32), OP.not_equal)
        tt(w(5), w(3), w(4), OP.mult)
        tt(w(6), w(2), w(5), OP.mult)
        tt(w(7), w(2), w(6), OP.subtract)
        ts(w(12, 2), X("LW", 0, 32), 2047, OP.not_equal)
        tt(w(14), w(12), w(13), OP.mult)
        tt(w(15), w(14), w(6), OP.mult)
        tt(w(10), X("AW", 16, 32), X("AW", 0, 16), OP.subtract)
        tt(w(11), X("LW", 16, 32), X("LW", 0, 16), OP.subtract)
        ts(w(26), w(5), -90, OP.mult, 99, OP.add)
        ts(w(27), w(5), -90, OP.mult, 99, OP.add)
        tt(w(16, 2), X("LW", 0, 32), X("DUF", 0, 32), OP.subtract)
        for i in range(2):
            tt(w(16 + i), w(16 + i), w(15), OP.mult)
        if not last:
            tt(w(18, 2), X("AW", 0, 32), X("DUF", 0, 32), OP.subtract)
            for i in range(2):
                tt(w(18 + i), w(18 + i), w(15), OP.mult)
        cur[0] = ""
        for i, src in enumerate(("SY", "SZ")):
            for r in range(16):
                mm(X("b5", 0, 32), X("WBW", 15 - r, 143 - r), X(src, 15 + 16 * r, 8192, 256), i == 0 and r == 0, i == 1 and r == 15)
        act(X("XW", X0 + YMO, X0 + YMO + 256), X("SY", 15, 4096, 16))
        act(X("XW", X0 + ZMO, X0 + ZMO + 256), X("SZ", 15, 4096, 16))
        for i, src in enumerate(("SY", "SZ")):
            for s in range(2):
                mm(X("b6", 0, 256), m128("IDN" if s else "IDB"), X(src, 4096 * s + 15, 4096 * s + 4096, 16), i + s == 0, i + s == 2)
        ts(X("GL", 0, 256), X("b6", 0, 256), 0, OP.is_gt)
        ts(X("GL", 256, 512), X("b6", 0, 256), 0, OP.is_lt)
        for r in range(16):
            mm(X("b2", 0, 32), X("WBB", 15 - r, 143 - r), X("GL", r, 512, 16), r == 0, r == 15)
        tc(X("SI", 0, 32), X("b5", 0, 32))
        bs = "BS2" if last else "BS1"
        ts(X("SI", 32, 48), X("SI", 0, 16), 127, OP.bitwise_and)
        tt(X(bs, 32, 48), X("SI", 32, 48), X("RBK", 16 * rnd, 16 * rnd + 16), OP.add)
        for i in range(3):
            tt(w(41 + i), X("LW" if i == 2 else "AW", 0, 16), X(bs, 16 * i, 16 * i + 16), OP.subtract)
            tt(w(44 + i), X("LW" if i == 2 else "AW", 16, 32), X(bs, 16 * i, 16 * i + 16), OP.subtract)
        tt(w(20, 2), X("b2", 0, 32), w(26, 2), OP.is_ge)
        for i in range(6):
            tt(w(48 + i), w(20 + i // 3), w(41 + i), OP.mult)
        tt(w(54, 3), w(48, 3), w(51, 3), OP.add)
        tt(w(57, 3), w(54, 3), X(bs, 0, 48), OP.add)
        ts(X("LT", 0, 48), w(57, 3), 0 if last else X0, OP.add)
        tt(w(25), w(20), w(21), OP.add)
        tt(w(34), w(25), w(16), OP.mult)
        tt(w(35), w(25), w(17), OP.mult)
        tt(w(36, 2), w(34, 2), X("DUF", 0, 32), OP.add)
        tc(X("LF", 0, 32), w(36, 2))
        add("V", "tc", IND(X("F", 0, 2576), X("LF", 0, 32)), [X("VALF", 0, 512)], (), 0.05 + 512 * 0.0031)
        tt(w(28), w(21), w(10), OP.mult)
        tt(w(32), w(28), X("AW", 0, 16), OP.add)
        if not last:
            tt(w(29), w(21), w(11), OP.mult)
            tt(w(33), w(29), X("LW", 0, 16), OP.add)
        twin = X("XW", X0, X0 + XEND) if last else X("XW", 0, X0 + R2O)
        for i in range(3):
            gat(X("TG", 256 * i, 256 * i + 256), IND(twin, X("LT", 16 * i, 16 * i + 16)), "AV")
        for i in range(3):
            mm(X("b3", 0, 256), m128("ID2" if i == 2 else "IDB"), X("TG", 256 * i, 256 * i + 256), i == 0, i == 2)
        tt(w(38), w(2), w(25), OP.mult)
        tt(w(39), w(38), w(7), OP.add)
        tt(w(60), w(32), X("DUX", 0, 16), OP.subtract)
        tt(w(61), w(60), w(39), OP.mult)
        tt(w(62), w(61), X("DUX", 0, 16), OP.add)
        tc(X("LX", 0, 16), w(62))
        ts(X("VI", 0, 256), X("b3", 0, 256), 0.25, OP.mult, -0.375, OP.add)
        add("W", "waitsent", X("XW", X0, X0 + 128), [], (rnd + 1,), 0)
        add("V", "tc", IND(X("XW", X0, X0 + YMO), X("LX", 0, 16)), [X("VI", 0, 256)], (), 0.05 + 256 * 0.0031)
        if last:
            dma("S", ("d", "yf"), X("F", 0, 2048, 1, 0, 128), "d7")
            for i in range(2):
                dma("SA"[i], ("d", "yx%d" % i), X("XW", X0 + 1024 * i, X0 + 1024 * i + 1024), "d%d" % (8 + i))
            break
        add("G", "send", None, [X("XW", X0, X0 + 128)], (2,), 1.0)
        add("N", "arrive", X("XW", X0 + R2O, X0 + XEND), [], (2,), 0)
        ts(w(63), w(33), 2047, OP.is_equal)
        tt(w(64), w(32), w(33), OP.subtract)
        tt(w(65), w(63), w(64), OP.mult)
        tt(w(66), w(65), w(33), OP.add)
        tc(X("LS", 0, 16), w(66))
        for s in range(2):
            tt(X("KDD", 64 * s, 64 * s + 64), X("KF", 256 * s, 256 * s + 64), X("DM", 0, 64), OP.mult)
        scan(X("KDS", 0, 128), X("RMH", 0, 128), X("KDD", 0, 128), OP.mult, OP.add)
        tc(X("KN", 0, 8), X("KDS", 15, 128, 16))
        tt(X("W", 1072, 1076), X("KN", 4, 8), X("KN", 0, 4), OP.subtract)
        tt(X("W", 1076, 1080), X("W", 1072, 1076), X("W", 336, 340), OP.mult)
        tt(X("LSI", 0, 4), X("W", 1076, 1080), X("KN", 0, 4), OP.add)
        tt(X("SI", 48, 64), X("SI", 0, 16), X("SI", 16, 32), OP.add)
        tt(X("LSI", 16, 32), X("SI", 48, 64), X("L977", 0, 16), OP.add)
        ts(X("LSI", 4, 16), X("LSI", 20, 32), 2047, OP.bitwise_and)
        tc(X("LS", 16, 32), X("LSI", 0, 16))
        mm(X("b1", 0, 256), m128("BLK"), X("PL", 256, 512), True, False)
        mm(X("b1", 0, 256), m128("NBLK"), X("PL", 0, 256), False, True)
        tt(X("TK", 0, 256), X("b1", 0, 256), X("OHS", 0, 256), OP.mult)
        ts(X("OHS", 256, 512), X("OHS", 256, 512), -1, OP.mult)
        tt(X("TK", 256, 512), X("b1", 0, 256), X("OHS", 256, 512), OP.mult)
        mm(X("b4", 0, 512), m128("IDH"), X("TK", 0, 512), True, False)
        mm(X("b4", 0, 512), m128("IDH"), X("KF", 0, 512), False, True)
        act(X("NK", 0, 512), X("b4", 0, 512))
        for i in range(2):
            tt(w(68 + i), w(25), w(18 + i), OP.mult)
        tt(w(70, 2), w(68, 2), X("DUF", 0, 32), OP.add)
        tc(X("LF", 32, 64), w(70, 2))
        add("V", "tc", IND(X("KD", 0, 2576), X("LF", 32, 64)), [X("NK", 0, 512)], (), 0.05 + 512 * 0.0031)
    return P


def deps(P):
    hist, n = {}, len(P)
    preds = [dict() for _ in P]
    for i, p in enumerate(P):
        for acc, wr in [(a, False) for a in p["r"]] + [(a, True) for a in p["w"]]:
            if acc[0] != "x":
                continue
            L = hist.setdefault(acc[1], [])
            for j, b, bw in L:
                if j == i:
                    continue
                if acc[1][0] == "b":
                    both = p["q"] == "T" and P[j]["q"] == "T"
                    if p["q"] != P[j]["q"] or ((wr or bw) and clash(acc, b) and not both):
                        preds[i][j] = True
                    else:
                        preds[i].setdefault(j, False)
                elif (wr or bw) and clash(acc, b):
                    preds[i][j] = True
            L.append((i, acc, wr))
    return preds


def order(P, preds):
    n = len(P)
    succ = [[] for _ in P]
    for i in range(n):
        for j in preds[i]:
            succ[j].append(i)
    prio = [0.0] * n
    for i in range(n - 1, -1, -1):
        lat = 2.0 if P[i]["what"] == "dma" else 0.0
        prio[i] = P[i]["cost"] + lat + max([prio[k] + WK for k in succ[i]] + [0.0])
    left = [len(p) for p in preds]
    ready = {i: 0.0 for i in range(n) if not left[i]}
    free = {q: 0.0 for q in "AVTGSNW"}
    seq, queue = [], [None] * n
    while ready:
        cand = []
        for i, t in ready.items():
            qs = P[i]["q"]
            q = min(qs, key=lambda z: max(free[z], t)) if len(qs) > 1 else qs
            cand.append((max(free[q], t), -prio[i] - BOOST.get(P[i]["b"], 0.0), i, q))
        first = min(cand)
        st, _, i, q = min((c for c in cand if c[3] == first[3] and c[0] <= first[0] + SLACK), key=lambda c: (c[1], c[0]))
        queue[i] = q
        end = st + P[i]["cost"]
        free[q] = end
        if P[i]["what"] == "dma":
            end += 2.0
        if P[i]["what"] == "arrive":
            end += 12.0
        P[i]["t"] = (st, end)
        seq.append(i)
        del ready[i]
        for k in succ[i]:
            left[k] -= 1
            if not left[k]:
                ready[k] = max([P[j]["t"][1] + (WK if preds[k][j] else 0.0) for j in preds[k]])
    return seq, queue, preds


PLAN = {}


def plan():
    if not PLAN:
        P = build()
        preds = deps(P)
        PLAN["p"] = (P,) + order(P, preds)
    return PLAN["p"]


def rank_program(g, core, T, topo):
    rank = T.rank_of(core)
    if rank is None:
        return
    P, seq, queue, preds = plan()
    eng = {"V": g.vector, "A": g.scalar, "T": g.tensor, "G": g, "S": g.sync}
    cores = list(T.cores)
    n = len(cores)

    def ap(a):
        if a[0] == "i":
            return ap(a[1]).indirect(ap(a[2]))
        if a[0] == "d":
            if a[1] == "yf":
                return T.yf[:]
            if a[1][:2] == "yx":
                i = int(a[1][2:])
                return T.yx[:, 1024 * i:1024 * i + 1024]
            return T[a[1]][:]
        _, name, lo, hi, st, p0, p1 = a
        return T[name][p0:p1, lo:hi] if st == 1 else T[name][p0:p1, lo:hi:st]

    def sc(s):
        return ap(s) if isinstance(s, tuple) else s

    count = {"V": 0, "A": 0, "T": 0, "G": 0}
    done, total = {}, {}
    seen = {q: {} for q in "VATGS"}

    def wait(q, sem, v):
        if seen[q].get(sem, 0) < v:
            seen[q][sem] = v
            eng[q].wait_ge(T.sem[sem], v)

    extra = {}
    for i in seq:
        p, q = P[i], queue[i]
        what, args = p["what"], p["args"]
        if what == "arrive":
            done[i] = [("arr%d" % args[0], ND * (n - 1))]
            total["arr%d" % args[0]] = ND * (n - 1)
            continue
        if what == "waitsent":
            done[i] = [s for j in preds[i] for s in done[j]] + [("sent%d" % args[0], ND)]
            continue
        need = {}
        for j, hard in preds[i].items():
            if hard:
                for sem, v in done[j]:
                    need[sem] = max(need.get(sem, 0), v)
        for sem in sorted(need):
            wait(q, sem, need[sem])
        out = p["out"] and ap(p["out"])
        ins = [ap(a) for a in p["ins"]]
        e = eng[q]
        if what == "dma":
            src = ins[0]
            if p["out"][1] == "yf":
                src = T.F[0::16, 0:2048]
            e.dma_start(out, src).then_inc(T.sem[args[0]], 16)
            done[i] = [(args[0], 16)]
            total[args[0]] = 16
            continue
        if what == "send":
            base = (0 if args[0] == 1 else X0 + R2O)
            others = [cores[(rank + d) % n] for d in range(1, n)]
            engines = [x for x in topo.engines(core, others[0]) if all(x in topo.engines(core, o) for o in others)][:ND]
            ids, dsts = [], []
            for o in others:
                rid, pid, _s = topo.addr(o)
                slot = (rank - T.rank_of(o) - 1) % n
                ids.append(DstId(rid=rid, pnc=pid))
                dsts.append(T.XW[:, base + 128 * slot:base + 128 * slot + 128])
            g.remote_dma_fused([RemoteDMATransfer(dst_ids=ids, dma_engine_mask=sum(1 << x for x in engines), remote_sem=T.sem["arr%d" % args[0]], srcs=[ins[0]], dsts=dsts)], local_sem=T.sem["sent%d" % args[0]])
            done[i] = [("sent%d" % args[0], ND)]
            total["sent%d" % args[0]] = ND
            continue
        if what == "tc" or (what == "gat" and q == "V"):
            h = e.tensor_copy(out, ins[0])
        elif what == "gat":
            h = e.activation(out, ins[0], AF.Copy)
        elif what == "count":
            h = e.activation(out, ins[0], AF.Copy, accum_out=ap(args[0]))
        elif what == "sq":
            h = e.activation(out, ins[0], AF.Square, bias=ins[1])
        elif what == "relu":
            h = e.activation(out, ins[0], AF.Relu)
        elif what == "act":
            h = e.activation(out, ins[0], AF.Identity, bias=ins[1]) if args[0] else e.activation(out, ins[0], AF.Copy)
        elif what == "tt":
            h = e.tensor_tensor(out, ins[0], ins[1], args[0])
        elif what == "ts":
            s1, o1, s2, o2 = args
            h = e.tensor_scalar(out, ins[0], sc(s1), None, o1) if o2 is None else e.tensor_scalar(out, ins[0], sc(s1), sc(s2), o1, o2)
        elif what == "scan":
            h = e.tensor_tensor_scan(out, ins[0], ins[1], 0.0, args[0], args[1])
        elif what == "mm":
            h = e.matmul(out, ins[0], ins[1], args[0], args[1])
        elif what == "tr":
            h = e.transpose(out, ins[0])
        elif what == "ms":
            h = e.memset(out, args[0])
        elif what == "iota":
            h = e.iota(out, args[0], args[2], args[1], allow_small_or_imprecise_dtypes=True)
        h.then_inc(T.sem["q" + q], 1)
        count[q] += 1
        done[i] = [("q" + q, count[q])]
    for q in "VATG":
        if count[q]:
            wait("S", "q" + q, count[q])
    for sem in sorted(total):
        wait("S", sem, total[sem])
